import numpy as np, ml_dtypes
CORES = [23,119,17,113]
N = 4
import mx_ref
BF = ml_dtypes.bfloat16
def pick(q, e):
    c = np.concatenate([q[0].reshape(128, -1, 4), np.zeros((128, 1, 4), np.uint8)], axis=1); s = np.concatenate([q[1], np.ones((16, 1), np.uint8)], axis=1)
    return (np.ascontiguousarray(c[:, e].reshape(128, -1)), np.ascontiguousarray(s[:, e]))
def join(*qs):
    return (np.concatenate([q[0] for q in qs], axis=1), np.concatenate([q[1] for q in qs], axis=1))
def put(q, e, v):
    c, s = q[0].reshape(128, -1, 4).copy(), q[1].copy(); c[:, e] = v[0].reshape(128, -1, 4); s[:, e] = v[1]
    return (c.reshape(128, -1), s)
def pk(c, s):
    return (np.ascontiguousarray(c), mx_ref.live(s))
def emit(q):
    return q[0], q[1]
def cut(t, i, w=512):
    return t[:, w * i:w * i + w]
def f(rng, *shape):
    return mx_ref.flush((rng.standard_normal(shape, dtype=np.float32) * np.exp2(rng.integers(-2, 3, shape[:-1] + (1,)))).astype(BF))
def wide(rng, *shape, cols=0):
    v = rng.standard_normal(shape, dtype=np.float32) * np.exp2(rng.integers(-12, 13, shape)).astype(np.float32)
    if cols: v *= np.repeat(np.exp2(rng.integers(-cols, cols + 1, shape[:-2] + (1, shape[-1] // 4))) * (rng.random(shape[:-2] + (1, shape[-1] // 4)) > 0.0625), 4, axis=-1).astype(np.float32)
    return mx_ref.flush(v.astype(BF))
P, K, S, O, L = 256, 16, 6, 3, 2
W = K * S
def gram(m, n):
    z = []
    for i in range(0, n, 128):
        e = np.arange(i, i + 128)
        z.append(mx_ref.matmul(pick(m, np.where(e < n, e, -1)), m))
    return np.concatenate(z)[:n]
def choose(m, num):
    n = len(num)
    g = gram(m, n)
    d = g[np.arange(n), np.arange(n)] + np.float32(0)
    g = np.abs(g)
    free, took = np.ones(n, bool), []
    for s in range(S):
        i = np.flatnonzero(free)
        best = i[np.lexsort((num[i], -d[i] + np.float32(0)))[:K]]
        took.append(best)
        free[best] = False
        i = np.flatnonzero(free)
        d[i] = d[i] - np.max(g[i][:, best], axis=1)
    return np.concatenate(took)
def astile(v):
    return np.ascontiguousarray(v.reshape(N, 128, 4, P).transpose(0, 1, 3, 2)).reshape(N, 128, 4 * P).astype(BF)
def weights(rng):
    return f(rng, N, 128, 512 * O)
def setup_inputs(rng):
    return {"x": f(rng, N, 128, 4 * P), "w": weights(rng)}
def setup_inputs_ties(rng):
    v = np.zeros((N, 512, P), np.float32)
    at = rng.permutation(512)
    for r in range(N):
        v[r][at[K + 1 + rng.permutation(P)], np.arange(P)] = 8
        v[r][at[0]] = np.concatenate([[1], 1 + rng.permutation(P - 1) % 2])
    s = int(rng.integers(N // 2, N))
    e = rng.permutation(P)[:K]
    v[s][:, e] = 0
    v[s][at[1:K + 1], e] = 16
    v[s][at[0], e] = 3
    v = v * (1 - 2 * rng.integers(0, 2, (N, 1, P))) * 2.0 ** int(rng.integers(-26, -20))
    return {"x": astile(v), "w": weights(rng)}
def close(rng, small):
    g = int(rng.integers(0, 8))
    rest = np.concatenate([np.arange(64 * g), np.arange(64 * g + 64, 512)])
    v = np.zeros((N, 512, P), np.float32)
    for r in range(N):
        v[r][rng.permutation(rest)[:P], np.arange(P)] = 3072
        v[r][64 * g:64 * g + 64] = small * (np.argsort(rng.random((64, P)), axis=0) < 8 + np.arange(P) * 48 // P)
    v = v * (1 - 2 * rng.integers(0, 2, (N, 1, P)))
    return {"x": astile(v), "w": weights(rng)}
def setup_inputs_near(rng):
    return close(rng, 1.0)
def setup_inputs_round(rng):
    return close(rng, 0.5)
def setup_inputs_deep(rng):
    v = np.full((N, 512, P), 2.0 ** 30)
    zeros = int(rng.integers(2, 4))
    for i, e in enumerate(rng.permutation(N * P)[:int(rng.integers(K // 2, K))]):
        v[e // P, :, e % P] = 0 if i < zeros else 2.0 ** 29 * (0.375 + 0.125 * rng.random()) * (1.5 + 0.5 * rng.random(512))
    v = v * (1 - 2 * rng.integers(0, 2, (1, 512, 1))) * (1 - 2 * rng.integers(0, 2, (N, 1, P))) + 0.0
    return {"x": astile(v.astype(np.float32)), "w": weights(rng)}
def setup_inputs_spread(rng):
    return {"x": wide(rng, N, 128, 4 * P, cols=6), "w": weights(rng)}
def check_inputs(d):
    b = []
    for k in ("x", "w"):
        v = np.abs(d[k].astype(np.float32))
        if not (np.isfinite(v).all() and ((v == 0) | (v >= 2.0 ** -30) & (v <= 2.0 ** 30)).all()): b.append("a value of " + k)
    return b
def reference(x, w):
    y, z = np.zeros((N, 128, O * W), np.float32), np.zeros((N, W, P), np.float32)
    wn, oc, osc = np.zeros((N, 1, W), np.float32), np.zeros((N, 128, 4 * W), np.uint8), np.zeros((N, 16, W), np.uint8)
    own = [mx_ref.quantize(np.ascontiguousarray(x[r])) for r in range(N)]
    num, win = [], []
    for r in range(N):
        at = choose(own[r], np.arange(P * r, P * r + P))
        num.append(P * r + at)
        win.append(pick(own[r], at))
    for t in range(L):
        num2, win2 = [], []
        for r in range(N):
            p = r ^ (1 << t)
            a, b = min(r, p), max(r, p)
            m, e = join(win[a], win[b]), np.concatenate([num[a], num[b]])
            at = choose(m, e)
            num2.append(e[at])
            win2.append(pick(m, at))
        num, win = num2, win2
    e = np.arange(128)
    for r in range(N):
        for o in range(O):
            y[r, :, o * W:o * W + W] = mx_ref.matmul(mx_ref.quantize(np.ascontiguousarray(cut(w[r], o))), win[r])
        z[r] = mx_ref.matmul(pick(win[r], np.where(e < W, e, -1)), own[r])[:W]
        wn[r, 0] = num[r]
        oc[r], osc[r] = emit(win[r])
    return {"y": y, "z": z, "wn": wn, "oc": oc, "osc": osc}

@@ -1,0 +1,439 @@
+from concourse.bass import DstId, RemoteDMATransfer
+from concourse.mybir import dt, AluOpType as A, AxisListType, ActivationFunctionType as F
+
+P, K, S, O = 256, 16, 6, 3
+W = K * S
+BIG = 1e29
+Q4, U8, F32, BF, U16, I32 = "float8_e4m3fn_x4", "uint8", "float32", "bfloat16", "uint16", "int32"
+
+
+def _sb(n, d):
+    return ("sbuf", [128, n], d)
+
+
+SCRATCH = {
+    "xt": _sb(4 * (P + 32), BF), "m0q": _sb(P + 32, Q4), "m0s": _sb(P + 32, U8),
+    "wt": _sb(512 * O, BF), "wq": _sb(128 * O, Q4), "ws": _sb(128 * O, U8),
+    "m1q": _sb(256, Q4), "m1s": _sb(256, U8), "m2q": _sb(256, Q4), "m2s": _sb(256, U8),
+    "m3q": _sb(128, Q4), "m3s": _sb(128, U8),
+    "ps": ("psum", [128, 4096], F32),
+    "ga": _sb(1280, F32), "nb": _sb(128, F32), "nr": _sb(256, F32), "gt": _sb(64, F32), "sc": _sb(64, F32),
+    "keep": _sb(64, F32), "negi": _sb(64, F32), "j16": _sb(64, F32), "zero": _sb(72, F32),
+    "eq0": _sb(516, BF), "eq1": _sb(388, BF), "tau0": _sb(516, BF), "tau1": _sb(388, BF),
+    "sig": _sb(516, BF), "eo": _sb(516, BF), "junk": _sb(512, BF),
+    "acc": _sb(2, F32), "rr": _sb(2, F32), "pre": _sb(64, F32), "tr": _sb(72, F32), "to": _sb(72, F32),
+    "r1": _sb(1, F32), "x1": _sb(1, F32), "ii": _sb(2, I32), "pf": _sb(2, F32),
+    "kc0": _sb(32, F32), "kc1": _sb(32, F32), "cb0": _sb(6, F32), "cb1": _sb(6, F32),
+    "pos0": _sb(4, F32), "pos1": _sb(4, F32),
+    "tmp0": _sb(16, F32), "tmp1": _sb(16, F32), "blk0": _sb(8, F32), "blk1": _sb(8, F32),
+    "df0": _sb(4, F32), "df1": _sb(4, F32),
+    "dg0": _sb(4, U16), "dg1": _sb(4, U16), "perm0": _sb(16, U16), "perm1": _sb(12, U16), "colo": _sb(2, U16),
+    "off0": _sb(30, U16), "off1": _sb(30, U16), "off2": _sb(30, U16),
+    "nat0": _sb(256, F32), "nat1": _sb(192, F32), "nat2": _sb(192, F32), "nat3": _sb(96, F32),
+    "tn1": _sb(104, F32), "tn2": _sb(104, F32), "pn": _sb(96, F32), "ncol": _sb(32, F32),
+    "sn1": _sb(2, U16), "sn2": _sb(2, U16), "ln1": _sb(2, U16), "ln2": _sb(2, U16),
+    "ysb": _sb(O * W, F32), "zsb": _sb(P, F32),
+}
+SEMAPHORES = ["cv", "cs", "ct", "cg", "lx", "lw", "ar1", "ar2", "an1", "an2", "ae1", "ae2", "sent",
+              "da1", "db1", "da2", "db2", "da3", "db3", "st"]
+
+
+def V(name, c0, c1, p0=0, p1=128, step=1):
+    return (name, p0, p1, c0, c1, step)
+
+
+def rank_program(g, core, T, topo):
+    rank = T.rank_of(core)
+    if rank is None:
+        return
+    queue = {"v": g.vector, "s": g.scalar, "t": g.tensor, "g": g, "y": g.sync}
+    own_sem = {"v": "cv", "s": "cs", "t": "ct", "g": "cg"}
+    count = {}
+    known = {k: {} for k in queue}
+    seen = {}
+
+    def ap(v):
+        return T[v[0]][v[1]:v[2], v[3]:v[4]:v[5]] if v[5] != 1 else T[v[0]][v[1]:v[2], v[3]:v[4]]
+
+    def box(v):
+        if v[0] == "ps":
+            return (0, 128, v[3] // 512 * 512, (v[4] + 511) // 512 * 512)
+        return (v[1], v[2], v[3], v[4])
+
+    def wait(q, h):
+        sem, val, clock = h
+        if known[q].get(sem, 0) < val:
+            queue[q].wait_ge(T.sem[sem], val)
+            known[q][sem] = val
+            for k in clock:
+                if known[q].get(k, 0) < clock[k]:
+                    known[q][k] = clock[k]
+
+    def note(v, writes, q, h):
+        b = box(v)
+        old = seen.get(v[0], [])
+        if writes and v[5] == 1:
+            old = [e for e in old if not (b[0] <= e[0] and e[1] <= b[1] and b[2] <= e[2] and e[3] <= b[3])]
+        seen[v[0]] = old + [b + (writes, q, h)]
+
+    def order(q, reads, writes):
+        need = {}
+        for vs, wr in ((reads, False), (writes, True)):
+            for v in vs:
+                b = box(v)
+                for e in seen.get(v[0], []):
+                    if b[0] < e[1] and e[0] < b[1] and b[2] < e[3] and e[2] < b[3]:
+                        if wr or e[4] or (v[0] == "ps" and e[5] != q):
+                            h = e[6]
+                            if h[0] not in need or need[h[0]][1] < h[1]:
+                                need[h[0]] = h
+        for k in sorted(need, key=lambda k: k == own_sem.get(q)):
+            wait(q, need[k])
+
+    def op(q, call, reads, writes, sem=None, inc=1):
+        order(q, reads, writes)
+        sem = sem or own_sem[q]
+        call().then_inc(T.sem[sem], inc)
+        count[sem] = count.get(sem, 0) + inc
+        h = (sem, count[sem], dict(known[q]))
+        for v in reads:
+            note(v, False, q, h)
+        for v in writes:
+            note(v, True, q, h)
+        return h
+
+    vec, act = g.vector, g.scalar
+
+    def isv(a):
+        return isinstance(a, tuple)
+
+    def ts(out, in0, s1, s2, op0, op1=None, off=None):
+        rd = [a for a in (in0, s1, s2, off) if isv(a)]
+        a0 = ap(in0) if off is None else ap(in0).indirect(ap(off))
+        a1, a2 = (ap(s1) if isv(s1) else s1), (ap(s2) if isv(s2) else s2)
+        if op1 is None:
+            return op("v", lambda: vec.tensor_scalar(ap(out), a0, a1, None, op0), rd, [out])
+        return op("v", lambda: vec.tensor_scalar(ap(out), a0, a1, a2, op0, op1), rd, [out])
+
+    def tt(out, in0, in1, o, off=None):
+        a0 = ap(in0) if off is None else ap(in0).indirect(ap(off))
+        return op("v", lambda: vec.tensor_tensor(ap(out), a0, ap(in1), o), [a for a in (in0, in1, off) if a], [out])
+
+    def cp(out, in0, off=None):
+        a0 = ap(in0) if off is None else ap(in0).indirect(ap(off))
+        return op("v", lambda: vec.tensor_copy(ap(out), a0), [a for a in (in0, off) if a], [out])
+
+    def ms(out, c):
+        return op("v", lambda: vec.memset(ap(out), c), [], [out])
+
+    def tp(out, in0):
+        return op("v", lambda: vec.transpose(ap(out), ap(in0)), [in0], [out])
+
+    def scan(out, d0, d1, o0, o1):
+        return op("v", lambda: vec.tensor_tensor_scan(ap(out), ap(d0), ap(d1), 0.0, o0, o1), [d0, d1], [out])
+
+    def ac(out, in0, func, off=None, bias=None, accum=None):
+        a0 = ap(in0) if off is None else ap(in0).indirect(ap(off))
+        kw = {}
+        if bias is not None:
+            kw["bias"], kw["scale"] = ap(bias), -1.0
+        if accum is not None:
+            kw["accum_out"] = ap(accum)
+        return op("s", lambda: act.activation(ap(out), a0, func, **kw), [a for a in (in0, off, bias) if a],
+                  [a for a in (out, accum) if a])
+
+    def iota(out, pattern, base, cm):
+        if SCRATCH[out[0]][2] == I32:
+            return op("g", lambda: g.iota(ap(out), pattern, base, cm), [], [out])
+        return op("g", lambda: g.iota(ap(out), pattern, base, cm, allow_small_or_imprecise_dtypes=True), [], [out])
+
+    def mm(bank, n, lq, l0, rq, r0=0):
+        a, b = (V(lq + "q", l0, l0 + 128), V(lq + "s", l0, l0 + 128)), (V(rq + "q", r0, r0 + n), V(rq + "s", r0, r0 + n))
+        out = V("ps", 512 * bank, 512 * bank + n)
+        return op("t", lambda: g.tensor.matmul_mx(ap(out), ap(a[0]), ap(a[1]), ap(b[0]), ap(b[1]), True, True),
+                  list(a + b), [out])
+
+    def pick(dst, d0, src, s0, n, off):
+        k = 16 * (off[4] - off[3])
+        o, i = V(dst + "q", d0, d0 + k), V(src + "q", s0, s0 + n)
+        op("v", lambda: vec.tensor_copy(ap(o).bitcast(dt.uint32), ap(i).bitcast(dt.uint32).indirect(ap(off))), [i, off], [o])
+        ac(V(dst + "s", d0, d0 + k), V(src + "s", s0, s0 + n), F.Copy, off=off)
+
+    def raw(v):
+        return ap(v).bitcast(dt.uint8) if SCRATCH[v[0]][2] == Q4 else ap(v)
+
+    def dma(q, out, v):
+        return op(q, lambda: queue[q].dma_start(out, raw(v)), [v], [], sem="st", inc=16)
+
+    def repeat(m, d0, s0, sem):
+        hs = []
+        for e in "qs":
+            o, i = V(m + e, d0, d0 + 32), V(m + e, s0, s0 + 32)
+            order("y", [i], [o])
+            g.sync.dma_start(raw(o), raw(i)).then_inc(T.sem[sem], 16)
+            hs.append((o, i))
+        h = (sem, 32, dict(known["y"]))
+        for o, i in hs:
+            note(i, False, "y", h)
+            note(o, True, "y", h)
+
+    sent = [0]
+
+    def bits(es):
+        return sum(1 << e for e in es)
+
+    def send(peer, pieces, sem):
+        order("g", [s for d, s in pieces], [])
+        rid, pid = topo.addr(peer)[:2]
+        es = topo.engines(core, peer)
+        if len(pieces) == 1:
+            g.remote_dma(raw(pieces[0][0]), raw(pieces[0][1]), T.sem[sem], T.sem.sent, pid, rid, bits(es))
+        else:
+            k = len(es) // len(pieces)
+            g.remote_dma_fused([RemoteDMATransfer(dst_ids=[DstId(rid=rid, pnc=pid)], dma_engine_mask=bits(es[k * i:k * i + k]),
+                                                  remote_sem=T.sem[sem], src=raw(s), dst=raw(d))
+                                for i, (d, s) in enumerate(pieces)], local_sem=T.sem.sent)
+        sent[0] += len(es)
+
+    peers = {c: T.cores[rank ^ (1 << (c - 1))] for c in (1, 2)}
+    for c in (1, 2):
+        ne = len(topo.engines(peers[c], core))
+        for e in "qs":
+            note(V("m%d%s" % (c, e), 32, 128), True, None, ("ar%d" % c, 4 * ne, {}))
+        note(V("ln%d" % c, 0, 2), True, None, ("ae%d" % c, ne, {}))
+        note(V("tn%d" % c, 100, 101), True, None, ("an%d" % c, ne, {}))
+
+    shape = {0: (256, (0, 1, 4, 5), (0, 1, 2, 3, 4, 5, 6, 7, 0), 0, (0, 2)),
+             1: (192, (0, 1, 4), (4, 0, 1, 2, 3, 4, 5, 5), 1, (1, 2))}
+
+    hx = ("lx", 32, {})
+    g.sync.dma_start(ap(V("xt", 0, 4 * P)), T.x[:]).then_inc(T.sem.lx, 16)
+    g.scalar.dma_start(ap(V("xt", 4 * P, 4 * P + 128)), T.x[:, 0:128]).then_inc(T.sem.lx, 16)
+    note(V("xt", 0, 4 * P + 128), True, "y", hx)
+    wait("y", hx)
+    op("y", lambda: g.sync.dma_start(T.wt[:], T.w[:]), [], [V("wt", 0, 512 * O)], sem="lw", inc=16)
+
+    iota(V("ii", 0, 2), [[0, 2]], 0, 1)
+    iota(V("pos0", 0, 4), [[128, 2], [32, 2]], 0, 1)
+    iota(V("cb0", 0, 6), [[256, 6]], -256, 0)
+    iota(V("nat0", 0, 256), [[1, 256]], P * rank, 0)
+    iota(V("j16", 0, 64), [[0, 4], [1, 16]], 0, 0)
+    iota(V("pos1", 0, 4), [[128, 2], [32, 2]], -32, 1)
+    iota(V("cb1", 0, 6), [[192, 6]], -192, 0)
+    ts(V("ii", 0, 1), V("ii", 0, 1), 31, None, A.bitwise_and)
+    ts(V("ii", 1, 2), V("ii", 1, 2), 15, None, A.bitwise_and)
+    cp(V("pf", 0, 2), V("ii", 0, 2))
+
+    def tables(z):
+        n, starts, seq, first, ranked = shape[z]
+        nw, t = len(starts), str(z)
+        for b, st in enumerate(starts):
+            for q in range(4):
+                if seq[st + q] != st + q - first:
+                    v = V("pos" + t, b, b + 1, 32 * q, 32 * q + 32)
+                    ts(v, v, float(32 * (seq[st + q] - st - q + first)), None, A.add)
+        ms(V("tau" + t, 0, n + 3, step=n + 2), 0.0)
+        ts(V("blk" + t, 0, nw), V("pos" + t, 0, nw), V("pf", 0, 1), None, A.subtract)
+        ms(V("eq" + t, n, n + 2), 0.0)
+        cp(V("blk" + t, nw, 2 * nw, 0, 64), V("blk" + t, 0, nw, 64, 128))
+        cp(V("blk" + t, nw, 2 * nw, 64, 128), V("blk" + t, 0, nw, 0, 64))
+        ms(V("tau" + t, n + 1, 2 * n + 4, step=n + 2), 1.0)
+        for hh in range(2):
+            ts(V("tmp" + t, hh, 4 * nw, step=2), V("blk" + t, 0, 2 * nw), V("pf", 1, 2), 16.0 * hh, A.add, A.add)
+        ms(V("eq" + t, 2 * n + 2, 2 * n + 4), 0.0)
+        cp(V("perm" + t, 0, 4 * nw), V("tmp" + t, 0, 4 * nw))
+        ms(V("cb" + t, 0, 6, step=5), 0.0)
+        if z == 0:
+            ts(V("df0", 0, 1), V("pos0", 0, 1), 512.0, None, A.add)
+            ts(V("df0", 1, 2), V("pos0", 0, 1), 640.0, None, A.add)
+            tt(V("df0", 2, 4), V("pos0", 2, 4), V("cb0", 1, 3), A.add)
+        else:
+            tt(V("df1", 0, nw), V("pos1", 0, nw), V("cb1", 1, 1 + nw), A.add)
+        ts(V("kc" + t, 0, 32), V("j16", 0, 32), 2.0, float(-n), A.mult, A.add)
+        cp(V("dg" + t, 0, nw), V("df" + t, 0, nw))
+
+    def signs(c):
+        z = min(c, 1)
+        n = shape[z][0]
+        for a in range(2):
+            ac(V("tau%d" % z, a * (n + 2) + 1, a * (n + 2) + 1 + n), V("nat%d" % c, 0, n), F.Sign,
+               off=V("perm%d" % z, 0, n // 16), bias=V("ncol", 16 * a, 16 * a + 1))
+
+    def multipliers(c):
+        z = min(c, 1)
+        n = shape[z][0]
+        tt(V("sig", 0, 2 * n + 3), V("tau%d" % z, 0, 2 * n + 3), V("tau%d" % z, 1, 2 * n + 4), A.mult)
+
+    ts(V("ncol", 0, 17, step=16), V("pos0", 0, 3, step=2), P * rank - 0.5, None, A.add)
+    tables(0)
+    signs(0)
+    ms(V("zero", 0, 72), 0.0)
+    ts(V("negi", 0, 64), V("j16", 0, 64), V("pf", 1, 2), -1.0, A.is_equal, A.mult)
+    ts(V("keep", 0, 64), V("j16", 0, 64), 0.0, None, A.is_gt)
+    multipliers(0)
+    op("v", lambda: vec.quantize_mx(T.m0q[:], T.m0s[:], T.xt[:]), [V("xt", 0, 4 * P + 128)],
+       [V("m0q", 0, P + 32), V("m0s", 0, P + 32)])
+
+    def choice(c):
+        z = min(c, 1)
+        n, starts, seq, first, ranked = shape[z]
+        nw, t = len(starts), str(z)
+        H, m0 = 32 * nw, 32 * first
+        m, nx, off = "m%d" % c, "m%d" % (c + 1), "off%d" % c
+        nat, natx, tnx = "nat%d" % c, "nat%d" % (c + 1), "tn%d" % (c + 1)
+        last = c == 2
+        place = (0, 32, 64) if last else (192, 160, 128)
+        placen = place if last else (160, 128, 96)
+        pair = [V(off, 10 * i + 4, 10 * i + 6) for i in range(3)]
+        npart = 96 if z else 128
+        posv = [V("pos" + t, b, b + 1, 0, npart) for b in ranked]
+        col = [V("nb", 32 * b, 32 * b + 1) for b in ranked]
+        peer, ar = peers.get(c + 1), "ar%d" % (c + 1)
+        turn = (2, 3, 0, 1) if c == 0 else (0, 1, 2)
+
+        if c:
+            tn = "tn%d" % c
+            cp(V(tn, 96, 98), V("ln%d" % c, 0, 2))
+            for b in range(2):
+                ts(V("pn", 32 * b + 32, 32 * b + 64), V("zero", 0, 32), V(tn, 96 + b, 97 + b), None, A.add)
+            tp(V(nat, 32, 96), V("pn", 32, 96))
+        for b in ((2, 0, 3, 1) if c == 0 else turn):
+            mm(b, n, m, 32 * starts[b], m, m0)
+        if c == 0:
+            for b in range(2):
+                cp(V("ga", 1024 + 128 * b, 1152 + 128 * b), V("ps", 544 * b, 544 * b + 128))
+        for b in turn:
+            ac(V("ga", b * n, b * n + n), V("ps", 512 * b, 512 * b + n), F.Abs)
+        if c:
+            ts(V("pn", 0, 32), V("zero", 0, 32), V(tn, 100, 101), None, A.add)
+            ts(V("ncol", 0, 32), V(tn, 0, 101), -0.5, None, A.add, off=V("colo", 0, 2))
+            tp(V(nat, 0, 32), V("pn", 0, 32))
+            signs(c)
+
+        for s in range(S):
+            win = V("ga", 0, nw * n)
+            if s == 0:
+                tt(V("gt", 0, 16 * nw), win if c else V("ga", 512, 1280), V("negi", 0, 16 * nw), A.mult, off=V("dg" + t, 0, nw))
+                scan(V("sc", 0, 16 * nw), V("keep", 0, 16 * nw), V("gt", 0, 16 * nw), A.mult, A.add)
+                for b in turn:
+                    st, q = starts[b], 0
+                    while q < 4:
+                        e = q + 1
+                        while e < 4 and seq[st + e] == seq[st + e - 1] + 1:
+                            e += 1
+                        c0 = b * n + 32 * seq[st + q]
+                        v = V("ga", c0, c0 + 32 * (e - q), 0, 32 * e)
+                        op("g", lambda: g.affine_select(ap(v), ap(v), [[-1, 32 * (e - q)]], A.not_equal, BIG, -32 * q, 1), [v], [v])
+                        q = e
+            else:
+                o0 = 10 * ((s - 1) // 2) + 6 * ((s - 1) % 2)
+                cp(V("gt", 0, 16 * nw), win, off=V(off, o0, o0 + nw))
+                if s in (2, 4):
+                    i = s // 2 - 1
+                    pick(nx, place[i], m, m0, n, pair[i])
+                    ac(V(natx, placen[i], placen[i] + 32), V(nat, 0, n), F.Identity, off=pair[i])
+                    if last and i == 0:
+                        repeat(nx, 96, 0, "da3")
+                        repeat(nx, 64, 0, "db3")
+                    elif last:
+                        mm(4, P, nx, 0, "m0")
+                        dma("y", T.oc[:, 0:256], V(nx + "q", 0, 64))
+                    elif i == 0:
+                        repeat(nx, 224, 192, "da%d" % (c + 1))
+                        send(peer, [(V(nx + "s", 96, 128), V(nx + "s", 192, 224))], ar)
+                    else:
+                        repeat(nx, 0, 160, "db%d" % (c + 1))
+                        send(peer, [(V(nx + "q", 64, 128), V(nx + "q", 160, 224))], ar)
+                if s == 5 and not last:
+                    pick(nx, 128, m, m0, n, V(off, 24, 25))
+                    send(peer, [(V(nx + "q", 32, 48), V(nx + "q", 128, 144))], ar)
+                scan(V("sc", 0, 16 * nw), V("keep", 0, 16 * nw), V("gt", 0, 16 * nw), A.mult, A.max)
+            for b in range(nw):
+                blk = V("nb", 32 * b, 32 * b + 32)
+                ts(blk, blk if s else V("zero", 0, 32), V("sc", 16 * b + 15, 16 * b + 16), None, A.add)
+            tp(V("nr", 0, H), V("nb", 0, H))
+            ac(V("nr", H, n, 0, 64), V("nr", 0, H, 64, 128), F.Copy)
+            ac(V("nr", H, n, 64, 128), V("nr", 0, H, 0, 64), F.Copy)
+            for a in range(2):
+                ac(V("junk", 256 * a, 256 * a + n), V("nr", 0, n), F.Sign, bias=col[a], accum=V("acc", a, a + 1))
+            for part in range(2):
+                for a in range(2):
+                    e0 = a * (n + 2) + part * H
+                    ts(V("eq" + t, e0, e0 + H), V("nr", part * H, part * H + H), col[a], None, A.is_equal)
+            if s == 0 and c:
+                multipliers(c)
+            scan(V("eo", 0, 2 * n + 3), V("sig", 0, 2 * n + 3), V("eq" + t, 0, 2 * n + 3), A.mult, A.add)
+            if s == 4 and last:
+                ac(V("zsb", 0, P, 0, 64), V("ps", 2048, 2048 + P, 0, 64), F.Copy)
+                dma("y", T.z[0:64, :], V("zsb", 0, P, 0, 64))
+            if s == 4 and not last:
+                tp(V(tnx, 32, 96), V(natx, 128, 192))
+            tt(V("rr", 0, 2), V("acc", 0, 2), V("eo", n, 2 * n + 3, step=n + 2), A.add)
+            if s == 4 and not last:
+                cp(V("sn%d" % (c + 1), 0, 2), V(tnx, 32, 96, step=32))
+                send(peer, [(V("ln%d" % (c + 1), 0, 2), V("sn%d" % (c + 1), 0, 2))], "ae%d" % (c + 1))
+            for a in range(2):
+                ts(V("pre", 32 * a, 32 * a + 32, 0, npart), V("kc" + t, 0, 32, 0, npart), V("rr", a, a + 1, 0, npart),
+                   posv[a], A.is_equal, A.mult)
+            tp(V("tr", 0, 64, 0, npart), V("pre", 0, 64, 0, npart))
+            o0, b0 = 10 * (s // 2) + 5 * (s % 2), 1 - s % 2
+            if z:
+                scan(V("to", 0, 70, 0, 96), V("zero", 0, 70, 0, 96), V("tr", 0, 70, 0, 96), A.add, A.add)
+                for q in range(4):
+                    ts(V(off, o0, o0 + 5, 32 * q, 32 * q + 32), V("to", 64 + b0, 69 + b0, 0, 32),
+                       V("to", 63, 64, 32, 64), V("to", 63, 64, 64, 96), A.add, A.add)
+                continue
+            op("v", lambda: vec.tensor_reduce(T.r1[:, 0:1], T.tr[:, 0:64], AxisListType.X, A.add), [V("tr", 0, 64)], [V("r1", 0, 1)])
+            r = [V("r1", 0, 1, 32 * q, 32 * q + 32) for q in range(4)]
+            ts(V("x1", 0, 1, 0, 32), r[1], r[2], r[3], A.add, A.add)
+            ts(V("x1", 0, 1, 32, 64), r[0], r[2], r[3], A.add, A.add)
+            for h in range(2):
+                ts(V(off, o0, o0 + 5, 64 * h, 64 * h + 64), V("cb" + t, b0, b0 + 5, 64 * h, 64 * h + 64),
+                   V("r1", 0, 1, 0, 64), V("x1", 0, 1, 0, 64), A.add, A.add)
+
+        if last:
+            pick(nx, 64, m, m0, n, pair[2])
+            cp(V(natx, 64, 96), V(nat, 0, n), off=pair[2])
+            return
+        pick(nx, 144, m, m0, n, V(off, 26, 27))
+        send(peer, [(V(nx + "q", 48, 64), V(nx + "q", 144, 160)), (V(nx + "s", 32, 96), V(nx + "s", 128, 192))], ar)
+        cp(V(natx, 96, 128), V(nat, 0, n), off=pair[2])
+        tp(V(tnx, 0, 32), V(natx, 96, 128))
+        send(peer, [(V(tnx, 100, 101), V(tnx, 0, 1))], "an%d" % (c + 1))
+
+    choice(0)
+    tables(1)
+    n1, starts1, seq1, first1, ranked1 = shape[1]
+    where = {0: 100, 1: 96, 2: 97, 3: 0, 4: 32, 5: 64}
+    for a, b in enumerate(ranked1):
+        for q in range(4):
+            ms(V("colo", a, a + 1, 32 * q, 32 * q + 32), where[seq1[starts1[b] + q]])
+    ms(V("tr", 64, 65), 0.0)
+    tt(V("tr", 65, 70), V("cb1", 1, 6), V("cb1", 0, 5), A.subtract)
+    for c in (1, 2):
+        ms(V("tn%d" % c, 98, 100), 0.0)
+    op("v", lambda: vec.quantize_mx(T.wq[:], T.ws[:], T.wt[:]), [V("wt", 0, 512 * O)], [V("wq", 0, 128 * O), V("ws", 0, 128 * O)])
+    choice(1)
+    choice(2)
+
+    def scales_out(q, k):
+        dma(q, T.osc[4 * k:4 * k + 4, :], V("m3s", 0, W, 32 * k, 32 * k + 4))
+
+    for o in range(O):
+        mm(5 + o, 128, "w", 128 * o, "m3")
+    mm(4, P, "m3", 0, "m0")
+    dma("y", T.oc[:, 256:4 * W], V("m3q", 64, W))
+    scales_out("y", 0)
+    dma("s", T.wn[:], V("nat3", 0, W, 0, 1))
+    for o in range(O):
+        cp(V("ysb", W * o, W * o + W), V("ps", 512 * (5 + o), 512 * (5 + o) + W))
+    ac(V("zsb", 0, P, 64, W), V("ps", 2048, 2048 + P, 64, W), F.Copy)
+    dma("y", T.y[:], V("ysb", 0, O * W))
+    dma("s", T.z[64:W, :], V("zsb", 0, P, 64, W))
+    scales_out("y", 1)
+    scales_out("s", 2)
+    scales_out("s", 3)
+    g.sync.wait_ge(T.sem.st, count["st"])
+    g.wait_ge(T.sem.sent, sent[0])
+    for k in own_sem:
+        wait("y", (own_sem[k], count[own_sem[k]], {}))

@@ -17,17 +17,16 @@ SCRATCH = {
     "m1q": _sb(256, Q4), "m1s": _sb(256, U8), "m2q": _sb(256, Q4), "m2s": _sb(256, U8),
     "m3q": _sb(128, Q4), "m3s": _sb(128, U8),
     "ps": ("psum", [128, 4096], F32),
-    "ga": _sb(1280, F32), "nb": _sb(128, F32), "nr": _sb(256, F32), "gt": _sb(64, F32), "sc": _sb(64, F32),
-    "keep": _sb(64, F32), "negi": _sb(64, F32), "j16": _sb(64, F32), "zero": _sb(72, F32),
+    "ga": _sb(1024, F32), "nb": _sb(128, F32), "nr": _sb(256, F32), "gt": _sb(64, F32), "sc": _sb(64, F32),
+    "dgo": _sb(512, F32), "keep": _sb(64, F32), "negi": _sb(128, F32), "j16": _sb(64, F32), "zero": _sb(104, F32),
     "eq0": _sb(516, BF), "eq1": _sb(388, BF), "tau0": _sb(516, BF), "tau1": _sb(388, BF),
     "sig": _sb(516, BF), "eo": _sb(516, BF), "junk": _sb(512, BF),
-    "acc": _sb(2, F32), "rr": _sb(2, F32), "pre": _sb(64, F32), "tr": _sb(72, F32), "to": _sb(72, F32),
-    "r1": _sb(1, F32), "x1": _sb(1, F32), "ii": _sb(2, I32), "pf": _sb(2, F32),
+    "acc": _sb(4, F32), "ks": _sb(64, F32), "pre": _sb(96, F32), "to": _sb(104, F32),
+    "tr0": _sb(104, F32), "tr1": _sb(72, F32), "ii": _sb(2, I32), "pf": _sb(2, F32), "pr": _sb(1, F32),
     "kc0": _sb(32, F32), "kc1": _sb(32, F32), "cb0": _sb(6, F32), "cb1": _sb(6, F32),
-    "pos0": _sb(4, F32), "pos1": _sb(4, F32),
+    "pos0": _sb(4, F32), "pos1": _sb(4, F32), "pb0": _sb(4, BF), "pb1": _sb(4, BF),
     "tmp0": _sb(16, F32), "tmp1": _sb(16, F32), "blk0": _sb(8, F32), "blk1": _sb(8, F32),
-    "df0": _sb(4, F32), "df1": _sb(4, F32),
-    "dg0": _sb(4, U16), "dg1": _sb(4, U16), "perm0": _sb(16, U16), "perm1": _sb(12, U16), "colo": _sb(2, U16),
+    "perm0": _sb(16, U16), "perm1": _sb(12, U16), "colo": _sb(2, U16),
     "off0": _sb(30, U16), "off1": _sb(30, U16), "off2": _sb(30, U16),
     "nat0": _sb(256, F32), "nat1": _sb(192, F32), "nat2": _sb(192, F32), "nat3": _sb(96, F32),
     "tn1": _sb(104, F32), "tn2": _sb(104, F32), "pn": _sb(96, F32), "ncol": _sb(32, F32),
@@ -115,9 +114,8 @@ def rank_program(g, core, T, topo):
             return op("v", lambda: vec.tensor_scalar(ap(out), a0, a1, None, op0), rd, [out])
         return op("v", lambda: vec.tensor_scalar(ap(out), a0, a1, a2, op0, op1), rd, [out])
 
-    def tt(out, in0, in1, o, off=None):
-        a0 = ap(in0) if off is None else ap(in0).indirect(ap(off))
-        return op("v", lambda: vec.tensor_tensor(ap(out), a0, ap(in1), o), [a for a in (in0, in1, off) if a], [out])
+    def tt(out, in0, in1, o):
+        return op("v", lambda: vec.tensor_tensor(ap(out), ap(in0), ap(in1), o), [in0, in1], [out])
 
     def cp(out, in0, off=None):
         a0 = ap(in0) if off is None else ap(in0).indirect(ap(off))
@@ -131,6 +129,13 @@ def rank_program(g, core, T, topo):
 
     def scan(out, d0, d1, o0, o1):
         return op("v", lambda: vec.tensor_tensor_scan(ap(out), ap(d0), ap(d1), 0.0, o0, o1), [d0, d1], [out])
+
+    def total(out, in0):
+        return op("v", lambda: vec.tensor_reduce(ap(out), ap(in0), AxisListType.X, A.add), [in0], [out])
+
+    def quant(m, src, c0, c1):
+        o, s, i = V(m + "q", c0, c1), V(m + "s", c0, c1), V(src, 4 * c0, 4 * c1)
+        return op("v", lambda: vec.quantize_mx(ap(o), ap(s), ap(i)), [i], [o, s])
 
     def ac(out, in0, func, off=None, bias=None, accum=None):
         a0 = ap(in0) if off is None else ap(in0).indirect(ap(off))
@@ -215,42 +220,45 @@ def rank_program(g, core, T, topo):
 
     iota(V("ii", 0, 2), [[0, 2]], 0, 1)
     iota(V("pos0", 0, 4), [[128, 2], [32, 2]], 0, 1)
-    iota(V("cb0", 0, 6), [[256, 6]], -256, 0)
     iota(V("nat0", 0, 256), [[1, 256]], P * rank, 0)
+    iota(V("pr", 0, 1), [[0, 1]], P * rank, 1)
     iota(V("j16", 0, 64), [[0, 4], [1, 16]], 0, 0)
+    iota(V("cb0", 0, 6), [[256, 6]], -256, 0)
     iota(V("pos1", 0, 4), [[128, 2], [32, 2]], -32, 1)
     iota(V("cb1", 0, 6), [[192, 6]], -192, 0)
     ts(V("ii", 0, 1), V("ii", 0, 1), 31, None, A.bitwise_and)
     ts(V("ii", 1, 2), V("ii", 1, 2), 15, None, A.bitwise_and)
+    ms(V("zero", 0, 104), 0.0)
+    ms(V("pre", 64, 96), 0.0)
+    ts(V("ncol", 0, 17, step=16), V("pos0", 0, 3, step=2), P * rank - 0.5, None, A.add)
     cp(V("pf", 0, 2), V("ii", 0, 2))
 
     def tables(z):
         n, starts, seq, first, ranked = shape[z]
-        nw, t = len(starts), str(z)
+        nw, t, tail = len(starts), str(z), (96, 64)[z]
+        calls = []
         for b, st in enumerate(starts):
             for q in range(4):
                 if seq[st + q] != st + q - first:
                     v = V("pos" + t, b, b + 1, 32 * q, 32 * q + 32)
-                    ts(v, v, float(32 * (seq[st + q] - st - q + first)), None, A.add)
-        ms(V("tau" + t, 0, n + 3, step=n + 2), 0.0)
-        ts(V("blk" + t, 0, nw), V("pos" + t, 0, nw), V("pf", 0, 1), None, A.subtract)
-        ms(V("eq" + t, n, n + 2), 0.0)
-        cp(V("blk" + t, nw, 2 * nw, 0, 64), V("blk" + t, 0, nw, 64, 128))
-        cp(V("blk" + t, nw, 2 * nw, 64, 128), V("blk" + t, 0, nw, 0, 64))
-        ms(V("tau" + t, n + 1, 2 * n + 4, step=n + 2), 1.0)
-        for hh in range(2):
-            ts(V("tmp" + t, hh, 4 * nw, step=2), V("blk" + t, 0, 2 * nw), V("pf", 1, 2), 16.0 * hh, A.add, A.add)
-        ms(V("eq" + t, 2 * n + 2, 2 * n + 4), 0.0)
-        cp(V("perm" + t, 0, 4 * nw), V("tmp" + t, 0, 4 * nw))
-        ms(V("cb" + t, 0, 6, step=5), 0.0)
-        if z == 0:
-            ts(V("df0", 0, 1), V("pos0", 0, 1), 512.0, None, A.add)
-            ts(V("df0", 1, 2), V("pos0", 0, 1), 640.0, None, A.add)
-            tt(V("df0", 2, 4), V("pos0", 2, 4), V("cb0", 1, 3), A.add)
-        else:
-            tt(V("df1", 0, nw), V("pos1", 0, nw), V("cb1", 1, 1 + nw), A.add)
-        ts(V("kc" + t, 0, 32), V("j16", 0, 32), 2.0, float(-n), A.mult, A.add)
-        cp(V("dg" + t, 0, nw), V("df" + t, 0, nw))
+                    calls.append((ts, v, v, float(32 * (seq[st + q] - st - q + first)), None, A.add))
+        calls += [
+            (ms, V("tau" + t, 0, n + 3, step=n + 2), 0.0),
+            (ms, V("eq" + t, n, n + 2), 0.0),
+            (ms, V("eq" + t, 2 * n + 2, 2 * n + 4), 0.0),
+            (ts, V("blk" + t, 0, nw), V("pos" + t, 0, nw), V("pf", 0, 1), None, A.subtract),
+            (ms, V("tau" + t, n + 1, 2 * n + 4, step=n + 2), 1.0),
+            (cp, V("pb" + t, 0, nw), V("pos" + t, 0, nw)),
+            (ms, V("tr" + t, tail, tail + 1), 0.0),
+            (cp, V("blk" + t, nw, 2 * nw, 0, 64), V("blk" + t, 0, nw, 64, 128)),
+            (cp, V("blk" + t, nw, 2 * nw, 64, 128), V("blk" + t, 0, nw, 0, 64)),
+            (ms, V("cb" + t, 0, 6, step=5), 0.0),
+            (ts, V("kc" + t, 0, 32), V("j16", 0, 32), 2.0, float(-n), A.mult, A.add),
+            (ts, V("tmp" + t, 0, 2 * nw), V("blk" + t, 0, 2 * nw), V("pf", 1, 2), None, A.add),
+            (tt, V("tr" + t, tail + 1, tail + 6), V("cb" + t, 1, 6), V("cb" + t, 0, 5), A.subtract),
+            (cp, V("perm" + t, 0, 4 * nw, step=2), V("tmp" + t, 0, 2 * nw)),
+            (ts, V("perm" + t, 1, 4 * nw, step=2), V("tmp" + t, 0, 2 * nw), 16.0, None, A.add)]
+        return calls
 
     def signs(c):
         z = min(c, 1)
@@ -259,25 +267,37 @@ def rank_program(g, core, T, topo):
             ac(V("tau%d" % z, a * (n + 2) + 1, a * (n + 2) + 1 + n), V("nat%d" % c, 0, n), F.Sign,
                off=V("perm%d" % z, 0, n // 16), bias=V("ncol", 16 * a, 16 * a + 1))
 
-    def multipliers(c):
+    def multipliers(c, a):
         z = min(c, 1)
         n = shape[z][0]
-        tt(V("sig", 0, 2 * n + 3), V("tau%d" % z, 0, 2 * n + 3), V("tau%d" % z, 1, 2 * n + 4), A.mult)
+        e0 = a * (n + 2)
+        tt(V("sig", e0, e0 + n + 1), V("tau%d" % z, e0, e0 + n + 1), V("tau%d" % z, e0 + 1, e0 + n + 2), A.mult)
 
-    ts(V("ncol", 0, 17, step=16), V("pos0", 0, 3, step=2), P * rank - 0.5, None, A.add)
-    tables(0)
+    for call in tables(0):
+        call[0](*call[1:])
     signs(0)
-    ms(V("zero", 0, 72), 0.0)
-    ts(V("negi", 0, 64), V("j16", 0, 64), V("pf", 1, 2), -1.0, A.is_equal, A.mult)
+    ts(V("negi", 0, 128), V("nat0", 0, 128), V("pr", 0, 1), -1.0, A.is_equal, A.mult)
     ts(V("keep", 0, 64), V("j16", 0, 64), 0.0, None, A.is_gt)
-    multipliers(0)
-    op("v", lambda: vec.quantize_mx(T.m0q[:], T.m0s[:], T.xt[:]), [V("xt", 0, 4 * P + 128)],
-       [V("m0q", 0, P + 32), V("m0s", 0, P + 32)])
+    quant("m0", "xt", 0, P + 32)
+
+    n1, starts1, seq1, first1, ranked1 = shape[1]
+    where = {0: 100, 1: 96, 2: 97, 3: 0, 4: 32, 5: 64}
+    spare = tables(1)
+    for a, b in enumerate(ranked1):
+        for q in range(4):
+            spare.append((ms, V("colo", a, a + 1, 32 * q, 32 * q + 32), where[seq1[starts1[b] + q]]))
+    spare += [(ms, V("tn%d" % c, 98, 100), 0.0) for c in (1, 2)]
+    spare += [(quant, "w", "wt", 128 * o, 128 * o + 128) for o in range(O)]
+
+    def between():
+        if spare:
+            call = spare.pop(0)
+            call[0](*call[1:])
 
     def choice(c):
         z = min(c, 1)
         n, starts, seq, first, ranked = shape[z]
-        nw, t = len(starts), str(z)
+        nw, t, tail = len(starts), str(z), (96, 64)[z]
         H, m0 = 32 * nw, 32 * first
         m, nx, off = "m%d" % c, "m%d" % (c + 1), "off%d" % c
         nat, natx, tnx = "nat%d" % c, "nat%d" % (c + 1), "tn%d" % (c + 1)
@@ -285,11 +305,18 @@ def rank_program(g, core, T, topo):
         place = (0, 32, 64) if last else (192, 160, 128)
         placen = place if last else (160, 128, 96)
         pair = [V(off, 10 * i + 4, 10 * i + 6) for i in range(3)]
-        npart = 96 if z else 128
-        posv = [V("pos" + t, b, b + 1, 0, npart) for b in ranked]
         col = [V("nb", 32 * b, 32 * b + 1) for b in ranked]
         peer, ar = peers.get(c + 1), "ar%d" % (c + 1)
-        turn = (2, 3, 0, 1) if c == 0 else (0, 1, 2)
+
+        def runs(b):
+            st, q, out = starts[b], 0, []
+            while q < 4:
+                e = q + 1
+                while e < 4 and seq[st + e] == seq[st + e - 1] + 1:
+                    e += 1
+                out.append((q, e, 32 * seq[st + q]))
+                q = e
+            return out
 
         if c:
             tn = "tn%d" % c
@@ -297,37 +324,29 @@ def rank_program(g, core, T, topo):
             for b in range(2):
                 ts(V("pn", 32 * b + 32, 32 * b + 64), V("zero", 0, 32), V(tn, 96 + b, 97 + b), None, A.add)
             tp(V(nat, 32, 96), V("pn", 32, 96))
-        for b in ((2, 0, 3, 1) if c == 0 else turn):
+        for b in range(nw):
             mm(b, n, m, 32 * starts[b], m, m0)
         if c == 0:
-            for b in range(2):
-                cp(V("ga", 1024 + 128 * b, 1152 + 128 * b), V("ps", 544 * b, 544 * b + 128))
-        for b in turn:
+            multipliers(0, 0)
+        for b in range(nw):
+            for q, e, c0 in runs(b):
+                tt(V("dgo", 128 * b + 32 * q, 128 * b + 32 * e), V("ps", 512 * b + c0, 512 * b + c0 + 32 * (e - q)),
+                   V("negi", 32 * q, 32 * e), A.mult)
+        for b in range(nw):
             ac(V("ga", b * n, b * n + n), V("ps", 512 * b, 512 * b + n), F.Abs)
+            for q, e, c0 in runs(b):
+                v = V("ga", b * n + c0, b * n + c0 + 32 * (e - q), 0, 32 * e)
+                op("g", lambda: g.affine_select(ap(v), ap(v), [[-1, 32 * (e - q)]], A.not_equal, BIG, -32 * q, 1), [v], [v])
+        for b in range(nw):
+            total(V("sc", 16 * b + 15, 16 * b + 16), V("dgo", 128 * b, 128 * b + 128))
         if c:
             ts(V("pn", 0, 32), V("zero", 0, 32), V(tn, 100, 101), None, A.add)
             ts(V("ncol", 0, 32), V(tn, 0, 101), -0.5, None, A.add, off=V("colo", 0, 2))
-            tp(V(nat, 0, 32), V("pn", 0, 32))
-            signs(c)
 
         for s in range(S):
-            win = V("ga", 0, nw * n)
-            if s == 0:
-                tt(V("gt", 0, 16 * nw), win if c else V("ga", 512, 1280), V("negi", 0, 16 * nw), A.mult, off=V("dg" + t, 0, nw))
-                scan(V("sc", 0, 16 * nw), V("keep", 0, 16 * nw), V("gt", 0, 16 * nw), A.mult, A.add)
-                for b in turn:
-                    st, q = starts[b], 0
-                    while q < 4:
-                        e = q + 1
-                        while e < 4 and seq[st + e] == seq[st + e - 1] + 1:
-                            e += 1
-                        c0 = b * n + 32 * seq[st + q]
-                        v = V("ga", c0, c0 + 32 * (e - q), 0, 32 * e)
-                        op("g", lambda: g.affine_select(ap(v), ap(v), [[-1, 32 * (e - q)]], A.not_equal, BIG, -32 * q, 1), [v], [v])
-                        q = e
-            else:
+            if s:
                 o0 = 10 * ((s - 1) // 2) + 6 * ((s - 1) % 2)
-                cp(V("gt", 0, 16 * nw), win, off=V(off, o0, o0 + nw))
+                cp(V("gt", 0, 16 * nw), V("ga", 0, nw * n), off=V(off, o0, o0 + nw))
                 if s in (2, 4):
                     i = s // 2 - 1
                     pick(nx, place[i], m, m0, n, pair[i])
@@ -344,52 +363,69 @@ def rank_program(g, core, T, topo):
                     else:
                         repeat(nx, 0, 160, "db%d" % (c + 1))
                         send(peer, [(V(nx + "q", 64, 128), V(nx + "q", 160, 224))], ar)
-                if s == 5 and not last:
+                elif s == 5 and not last:
                     pick(nx, 128, m, m0, n, V(off, 24, 25))
                     send(peer, [(V(nx + "q", 32, 48), V(nx + "q", 128, 144))], ar)
+                else:
+                    between()
                 scan(V("sc", 0, 16 * nw), V("keep", 0, 16 * nw), V("gt", 0, 16 * nw), A.mult, A.max)
+                between()
             for b in range(nw):
                 blk = V("nb", 32 * b, 32 * b + 32)
                 ts(blk, blk if s else V("zero", 0, 32), V("sc", 16 * b + 15, 16 * b + 16), None, A.add)
+            if s == 0 and c:
+                tp(V(nat, 0, 32), V("pn", 0, 32))
+                signs(c)
+            elif s == 0:
+                multipliers(0, 1)
+            else:
+                between()
             tp(V("nr", 0, H), V("nb", 0, H))
-            ac(V("nr", H, n, 0, 64), V("nr", 0, H, 64, 128), F.Copy)
-            ac(V("nr", H, n, 64, 128), V("nr", 0, H, 0, 64), F.Copy)
-            for a in range(2):
-                ac(V("junk", 256 * a, 256 * a + n), V("nr", 0, n), F.Sign, bias=col[a], accum=V("acc", a, a + 1))
+            tp(V("nr", H, n, 0, 64), V("nb", 0, H, 64, 128))
+            tp(V("nr", H, n, 64, 128), V("nb", 0, H, 0, 64))
+            for part in range(2):
+                for a in range(2):
+                    ac(V("junk", 256 * a + part * H, 256 * a + part * H + H), V("nr", part * H, part * H + H), F.Sign,
+                       bias=col[a], accum=V("acc", 2 * a + part, 2 * a + part + 1))
             for part in range(2):
                 for a in range(2):
                     e0 = a * (n + 2) + part * H
                     ts(V("eq" + t, e0, e0 + H), V("nr", part * H, part * H + H), col[a], None, A.is_equal)
             if s == 0 and c:
-                multipliers(c)
-            scan(V("eo", 0, 2 * n + 3), V("sig", 0, 2 * n + 3), V("eq" + t, 0, 2 * n + 3), A.mult, A.add)
+                multipliers(c, 0)
+                multipliers(c, 1)
+            else:
+                between()
+            for a in range(2):
+                e0 = a * (n + 2)
+                scan(V("eo", e0, e0 + n + 1), V("sig", e0, e0 + n + 1), V("eq" + t, e0, e0 + n + 1), A.mult, A.add)
+                ts(V("ks", 32 * a, 32 * a + 32), V("kc" + t, 0, 32), V("acc", 2 * a, 2 * a + 1), V("acc", 2 * a + 1, 2 * a + 2),
+                   A.subtract, A.subtract)
             if s == 4 and last:
                 ac(V("zsb", 0, P, 0, 64), V("ps", 2048, 2048 + P, 0, 64), F.Copy)
                 dma("y", T.z[0:64, :], V("zsb", 0, P, 0, 64))
             if s == 4 and not last:
                 tp(V(tnx, 32, 96), V(natx, 128, 192))
-            tt(V("rr", 0, 2), V("acc", 0, 2), V("eo", n, 2 * n + 3, step=n + 2), A.add)
+            else:
+                between()
+            for a in range(2):
+                e1 = a * (n + 2) + n
+                for p0, p1, d0, c0 in ((0, 96, 0, 32 * a), (96, 128, 32 * a, 64))[:2 - z]:
+                    ts(V("pre", c0, c0 + 32, d0, d0 + p1 - p0), V("ks", 32 * a, 32 * a + 32, p0, p1),
+                       V("eo", e1, e1 + 1, p0, p1), V("pb" + t, ranked[a], ranked[a] + 1, p0, p1), A.is_equal, A.mult)
             if s == 4 and not last:
                 cp(V("sn%d" % (c + 1), 0, 2), V(tnx, 32, 96, step=32))
                 send(peer, [(V("ln%d" % (c + 1), 0, 2), V("sn%d" % (c + 1), 0, 2))], "ae%d" % (c + 1))
-            for a in range(2):
-                ts(V("pre", 32 * a, 32 * a + 32, 0, npart), V("kc" + t, 0, 32, 0, npart), V("rr", a, a + 1, 0, npart),
-                   posv[a], A.is_equal, A.mult)
-            tp(V("tr", 0, 64, 0, npart), V("pre", 0, 64, 0, npart))
-            o0, b0 = 10 * (s // 2) + 5 * (s % 2), 1 - s % 2
-            if z:
-                scan(V("to", 0, 70, 0, 96), V("zero", 0, 70, 0, 96), V("tr", 0, 70, 0, 96), A.add, A.add)
-                for q in range(4):
-                    ts(V(off, o0, o0 + 5, 32 * q, 32 * q + 32), V("to", 64 + b0, 69 + b0, 0, 32),
-                       V("to", 63, 64, 32, 64), V("to", 63, 64, 64, 96), A.add, A.add)
-                continue
-            op("v", lambda: vec.tensor_reduce(T.r1[:, 0:1], T.tr[:, 0:64], AxisListType.X, A.add), [V("tr", 0, 64)], [V("r1", 0, 1)])
-            r = [V("r1", 0, 1, 32 * q, 32 * q + 32) for q in range(4)]
-            ts(V("x1", 0, 1, 0, 32), r[1], r[2], r[3], A.add, A.add)
-            ts(V("x1", 0, 1, 32, 64), r[0], r[2], r[3], A.add, A.add)
-            for h in range(2):
-                ts(V(off, o0, o0 + 5, 64 * h, 64 * h + 64), V("cb" + t, b0, b0 + 5, 64 * h, 64 * h + 64),
-                   V("r1", 0, 1, 0, 64), V("x1", 0, 1, 0, 64), A.add, A.add)
+            else:
+                between()
+            tp(V("tr" + t, 0, tail, 0, 96), V("pre", 0, tail, 0, 96))
+            between()
+            scan(V("to", 0, tail + 6, 0, 96), V("zero", 0, tail + 6, 0, 96), V("tr" + t, 0, tail + 6, 0, 96), A.add, A.add)
+            between()
+            o0, b0 = 10 * (s // 2) + 5 * (s % 2), tail + 1 - s % 2
+            for q in range(4):
+                ts(V(off, o0, o0 + 5, 32 * q, 32 * q + 32), V("to", b0, b0 + 5, 0, 32),
+                   V("to", tail - 1, tail, 32, 64), V("to", tail - 1, tail, 64, 96), A.add, A.add)
 
         if last:
             pick(nx, 64, m, m0, n, pair[2])
@@ -400,21 +436,11 @@ def rank_program(g, core, T, topo):
         cp(V(natx, 96, 128), V(nat, 0, n), off=pair[2])
         tp(V(tnx, 0, 32), V(natx, 96, 128))
         send(peer, [(V(tnx, 100, 101), V(tnx, 0, 1))], "an%d" % (c + 1))
+        while spare:
+            between()
 
-    choice(0)
-    tables(1)
-    n1, starts1, seq1, first1, ranked1 = shape[1]
-    where = {0: 100, 1: 96, 2: 97, 3: 0, 4: 32, 5: 64}
-    for a, b in enumerate(ranked1):
-        for q in range(4):
-            ms(V("colo", a, a + 1, 32 * q, 32 * q + 32), where[seq1[starts1[b] + q]])
-    ms(V("tr", 64, 65), 0.0)
-    tt(V("tr", 65, 70), V("cb1", 1, 6), V("cb1", 0, 5), A.subtract)
-    for c in (1, 2):
-        ms(V("tn%d" % c, 98, 100), 0.0)
-    op("v", lambda: vec.quantize_mx(T.wq[:], T.ws[:], T.wt[:]), [V("wt", 0, 512 * O)], [V("wq", 0, 128 * O), V("ws", 0, 128 * O)])
-    choice(1)
-    choice(2)
+    for c in range(3):
+        choice(c)
 
     def scales_out(q, k):
         dma(q, T.osc[4 * k:4 * k + 4, :], V("m3s", 0, W, 32 * k, 32 * k + 4))

@@ -18,9 +18,14 @@ SCRATCH = {
     "m3q": _sb(128, Q4), "m3s": _sb(128, U8),
     "ps": ("psum", [128, 4096], F32),
     "ga": _sb(1024, F32), "nb": _sb(128, F32), "nr": _sb(256, F32), "gt": _sb(64, F32), "sc": _sb(64, F32),
-    "dgo": _sb(512, F32), "keep": _sb(64, F32), "negi": _sb(128, F32), "j16": _sb(64, F32), "zero": _sb(104, F32),
+    "dgo": _sb(512, F32), "dg": _sb(4, F32), "keep": _sb(64, F32), "negi": _sb(128, F32),
+    "j16": _sb(64, F32), "zero": _sb(104, F32),
     "eq0": _sb(516, BF), "eq1": _sb(388, BF), "tau0": _sb(516, BF), "tau1": _sb(388, BF),
     "sig": _sb(516, BF), "eo": _sb(516, BF), "junk": _sb(512, BF),
+    "eqm": _sb(66, BF), "taum": _sb(66, BF), "sigm": _sb(66, BF), "kcm": _sb(32, F32), "trm": _sb(40, F32),
+    "pbm": _sb(2, BF), "colm": _sb(2, F32), "dgm": _sb(128, F32), "dm": _sb(1, F32), "pnm": _sb(32, F32),
+    "nbm": _sb(64, F32), "nrm": _sb(64, F32), "junkm": _sb(64, BF), "accm": _sb(1, F32), "eom": _sb(66, BF),
+    "ksm": _sb(32, F32), "prem": _sb(32, F32), "tom": _sb(40, F32), "lr": _sb(16, F32),
     "acc": _sb(4, F32), "ks": _sb(64, F32), "pre": _sb(96, F32), "to": _sb(104, F32),
     "tr0": _sb(104, F32), "tr1": _sb(72, F32), "ii": _sb(2, I32), "pf": _sb(2, F32), "pr": _sb(1, F32),
     "kc0": _sb(32, F32), "kc1": _sb(32, F32), "cb0": _sb(6, F32), "cb1": _sb(6, F32),
@@ -29,12 +34,13 @@ SCRATCH = {
     "perm0": _sb(16, U16), "perm1": _sb(12, U16), "colo": _sb(2, U16),
     "off0": _sb(30, U16), "off1": _sb(30, U16), "off2": _sb(30, U16),
     "nat0": _sb(256, F32), "nat1": _sb(192, F32), "nat2": _sb(192, F32), "nat3": _sb(96, F32),
-    "tn1": _sb(104, F32), "tn2": _sb(104, F32), "pn": _sb(96, F32), "ncol": _sb(32, F32),
+    "tn1": _sb(104, F32), "tn2": _sb(104, F32), "pn": _sb(64, F32), "ncol": _sb(32, F32),
     "sn1": _sb(2, U16), "sn2": _sb(2, U16), "ln1": _sb(2, U16), "ln2": _sb(2, U16),
+    "sa1": _sb(2, U16), "sa2": _sb(2, U16), "la1": _sb(2, U16), "la2": _sb(2, U16),
     "ysb": _sb(O * W, F32), "zsb": _sb(P, F32),
 }
-SEMAPHORES = ["cv", "cs", "ct", "cg", "lx", "lw", "ar1", "ar2", "an1", "an2", "ae1", "ae2", "sent",
-              "da1", "db1", "da2", "db2", "da3", "db3", "st"]
+SEMAPHORES = ["cv", "cs", "ct", "cg", "lx", "lw", "ar1", "ar2", "ab1", "ab2", "an1", "an2", "ae1", "ae2", "sent",
+              "da1", "db1", "dc1", "dd1", "da2", "db2", "dc2", "dd2", "da3", "db3", "st"]
 
 
 def V(name, c0, c1, p0=0, p1=128, step=1):
@@ -204,9 +210,10 @@ def rank_program(g, core, T, topo):
     for c in (1, 2):
         ne = len(topo.engines(peers[c], core))
         for e in "qs":
-            note(V("m%d%s" % (c, e), 32, 128), True, None, ("ar%d" % c, 4 * ne, {}))
-        note(V("ln%d" % c, 0, 2), True, None, ("ae%d" % c, ne, {}))
-        note(V("tn%d" % c, 100, 101), True, None, ("an%d" % c, ne, {}))
+            note(V("m%d%s" % (c, e), 32, 96), True, None, ("ar%d" % c, 3 * ne, {}))
+            note(V("m%d%s" % (c, e), 96, 128), True, None, ("ab%d" % c, 2 * ne, {}))
+        note(V("la%d" % c, 0, 2), True, None, ("ae%d" % c, ne, {}))
+        note(V("ln%d" % c, 0, 2), True, None, ("an%d" % c, ne, {}))
 
     shape = {0: (256, (0, 1, 4, 5), (0, 1, 2, 3, 4, 5, 6, 7, 0), 0, (0, 2)),
              1: (192, (0, 1, 4), (4, 0, 1, 2, 3, 4, 5, 5), 1, (1, 2))}
@@ -257,6 +264,7 @@ def rank_program(g, core, T, topo):
             (ts, V("tmp" + t, 0, 2 * nw), V("blk" + t, 0, 2 * nw), V("pf", 1, 2), None, A.add),
             (tt, V("tr" + t, tail + 1, tail + 6), V("cb" + t, 1, 6), V("cb" + t, 0, 5), A.subtract),
             (cp, V("perm" + t, 0, 4 * nw, step=2), V("tmp" + t, 0, 2 * nw)),
+            (ts, V("kcm", 0, 32), V("j16", 0, 32), 2.0, -64.0, A.mult, A.add) if z else (ms, V("taum", 0, 1), 0.0),
             (ts, V("perm" + t, 1, 4 * nw, step=2), V("tmp" + t, 0, 2 * nw), 16.0, None, A.add)]
         return calls
 
@@ -281,18 +289,48 @@ def rank_program(g, core, T, topo):
     quant("m0", "xt", 0, P + 32)
 
     n1, starts1, seq1, first1, ranked1 = shape[1]
-    where = {0: 100, 1: 96, 2: 97, 3: 0, 4: 32, 5: 64}
-    spare = tables(1)
+    where = {0: 96, 1: 97, 2: 98, 3: 0, 4: 32, 5: 64}
+    early = (64, 160)
+    flat = tables(1)
     for a, b in enumerate(ranked1):
         for q in range(4):
-            spare.append((ms, V("colo", a, a + 1, 32 * q, 32 * q + 32), where[seq1[starts1[b] + q]]))
-    spare += [(ms, V("tn%d" % c, 98, 100), 0.0) for c in (1, 2)]
-    spare += [(quant, "w", "wt", 128 * o, 128 * o + 128) for o in range(O)]
+            flat.append((ms, V("colo", a, a + 1, 32 * q, 32 * q + 32), where[seq1[starts1[b] + q]]))
+    flat += [(ts, V("pbm", 0, 1, 32 * i, 32 * i + 32), V("pf", 0, 1, 32 * i, 32 * i + 32), float(early[i]), None, A.add)
+             for i in range(2)]
+    flat += [(cp, V("trm", 32, 38), V("tr1", 64, 70)), (ms, V("eqm", 64, 66), 0.0), (ms, V("taum", 65, 66), 1.0)]
+    spare = [flat[i:i + 2] for i in range(0, len(flat), 2)]
 
     def between():
         if spare:
-            call = spare.pop(0)
-            call[0](*call[1:])
+            for call in spare.pop(0):
+                call[0](*call[1:])
+
+    def first_step(c):
+        tn, nat, off, la = "tn%d" % c, "nat%d" % c, "off%d" % c, "la%d" % c
+        src = [V("dm", 0, 1, 96 * i, 96 * i + 32) for i in range(2)]
+        wide = [(ts, V("nbm", 32 * i, 32 * i + 32, 32 * q, 32 * q + 32), V("zero", 0, 32, 96 * i, 96 * i + 32), src[i], None, A.add)
+                for i in range(2) for q in range(2)]
+        return [
+            [(cp, V(tn, 98, 99), V(la, 0, 1)),
+             (ts, V("colm", 1, 2, 32, 64), V(tn, 64, 65, 32, 64), -0.5, None, A.add),
+             (ts, V("colm", 1, 2, 0, 32), V(la, 0, 1, 0, 32), -0.5, None, A.add)],
+            [(tt, V("dgm", 0, 128), V("ps", 2560, 2688), V("negi", 0, 128), A.mult),
+             (ts, V("pnm", 0, 32), V("zero", 0, 32), V(tn, 98, 99), None, A.add)],
+            [(total, V("dm", 0, 1), V("dgm", 0, 128)), (tp, V(nat, 64, 96), V("pnm", 0, 32))],
+            wide[:3] + [(ac, V("taum", 1 + 32 * i, 33 + 32 * i, 0, 64), V(nat, early[i], early[i] + 32, 0, 64), F.Sign, None,
+                         V("colm", 1, 2, 0, 64)) for i in range(2)],
+            wide[3:] + [(cp, V("colm", 0, 1, 32 * i, 32 * i + 32), src[i]) for i in range(2)],
+            [(tp, V("nrm", 0, 64, 0, 64), V("nbm", 0, 64, 0, 64)),
+             (tt, V("sigm", 0, 65, 0, 64), V("taum", 0, 65, 0, 64), V("taum", 1, 66, 0, 64), A.mult)],
+            [(ac, V("junkm", 0, 64, 0, 64), V("nrm", 0, 64, 0, 64), F.Sign, None, V("colm", 0, 1, 0, 64), V("accm", 0, 1, 0, 64)),
+             (ts, V("eqm", 0, 64, 0, 64), V("nrm", 0, 64, 0, 64), V("colm", 0, 1, 0, 64), None, A.is_equal)],
+            [(scan, V("eom", 0, 65, 0, 64), V("sigm", 0, 65, 0, 64), V("eqm", 0, 65, 0, 64), A.mult, A.add)],
+            [(ts, V("ksm", 0, 32, 0, 64), V("kcm", 0, 32, 0, 64), V("accm", 0, 1, 0, 64), None, A.subtract)],
+            [(ts, V("prem", 0, 32, 0, 64), V("ksm", 0, 32, 0, 64), V("eom", 64, 65, 0, 64), V("pbm", 0, 1, 0, 64), A.is_equal, A.mult)],
+            [(tp, V("trm", 0, 32, 0, 64), V("prem", 0, 32, 0, 64))],
+            [(scan, V("tom", 0, 38, 0, 64), V("zero", 0, 38, 0, 64), V("trm", 0, 38, 0, 64), A.add, A.add)],
+            [(ts, V(off, 0, 5, 32 * q, 32 * q + 32), V("tom", 33, 38, 0, 32), V("tom", 31, 32, 32, 64), None, A.add) for q in range(2)],
+            [(ts, V(off, 0, 5, 32 * q, 32 * q + 32), V("tom", 33, 38, 0, 32), V("tom", 31, 32, 32, 64), None, A.add) for q in (2, 3)]]
 
     def choice(c):
         z = min(c, 1)
@@ -306,7 +344,7 @@ def rank_program(g, core, T, topo):
         placen = place if last else (160, 128, 96)
         pair = [V(off, 10 * i + 4, 10 * i + 6) for i in range(3)]
         col = [V("nb", 32 * b, 32 * b + 1) for b in ranked]
-        peer, ar = peers.get(c + 1), "ar%d" % (c + 1)
+        peer, ar, ab = peers.get(c + 1), "ar%d" % (c + 1), "ab%d" % (c + 1)
 
         def runs(b):
             st, q, out = starts[b], 0, []
@@ -318,32 +356,48 @@ def rank_program(g, core, T, topo):
                 q = e
             return out
 
+        def diagonal(b):
+            for q, e, c0 in runs(b):
+                tt(V("dgo", 128 * b + 32 * q, 128 * b + 32 * e), V("ps", 512 * b + c0, 512 * b + c0 + 32 * (e - q)),
+                   V("negi", 32 * q, 32 * e), A.mult)
+
+        def magnitudes(b):
+            ac(V("ga", b * n, b * n + n), V("ps", 512 * b, 512 * b + n), F.Abs)
+
+        def raise_diagonal(b):
+            for q, e, c0 in runs(b):
+                v = V("ga", b * n + c0, b * n + c0 + 32 * (e - q), 0, 32 * e)
+                op("g", lambda: g.affine_select(ap(v), ap(v), [[-1, 32 * (e - q)]], A.not_equal, BIG, -32 * q, 1), [v], [v])
+
+        def diagonal_sum(b):
+            total(V("dg", b, b + 1), V("dgo", 128 * b, 128 * b + 128))
+
         if c:
             tn = "tn%d" % c
-            cp(V(tn, 96, 98), V("ln%d" % c, 0, 2))
-            for b in range(2):
-                ts(V("pn", 32 * b + 32, 32 * b + 64), V("zero", 0, 32), V(tn, 96 + b, 97 + b), None, A.add)
-            tp(V(nat, 32, 96), V("pn", 32, 96))
+            ts(V("lr", 0, 16), V("nat0", 0, n), -float(P * rank), None, A.add, off=V(off, 0, 1))
+            for b in range(nw):
+                ts(V("gt", 16 * b, 16 * b + 16), V("lr", 0, 16), V("pos1", b, b + 1), BIG, A.is_equal, A.mult)
+            scan(V("sc", 0, 16 * nw), V("keep", 0, 16 * nw), V("gt", 0, 16 * nw), A.mult, A.max)
+            for b in range(nw):
+                ts(V("nb", 32 * b, 32 * b + 32), V("zero", 0, 32), V("sc", 16 * b + 15, 16 * b + 16), None, A.add)
         for b in range(nw):
             mm(b, n, m, 32 * starts[b], m, m0)
         if c == 0:
             multipliers(0, 0)
-        for b in range(nw):
-            for q, e, c0 in runs(b):
-                tt(V("dgo", 128 * b + 32 * q, 128 * b + 32 * e), V("ps", 512 * b + c0, 512 * b + c0 + 32 * (e - q)),
-                   V("negi", 32 * q, 32 * e), A.mult)
-        for b in range(nw):
-            ac(V("ga", b * n, b * n + n), V("ps", 512 * b, 512 * b + n), F.Abs)
-            for q, e, c0 in runs(b):
-                v = V("ga", b * n + c0, b * n + c0 + 32 * (e - q), 0, 32 * e)
-                op("g", lambda: g.affine_select(ap(v), ap(v), [[-1, 32 * (e - q)]], A.not_equal, BIG, -32 * q, 1), [v], [v])
-        for b in range(nw):
-            total(V("sc", 16 * b + 15, 16 * b + 16), V("dgo", 128 * b, 128 * b + 128))
-        if c:
-            ts(V("pn", 0, 32), V("zero", 0, 32), V(tn, 100, 101), None, A.add)
-            ts(V("ncol", 0, 32), V(tn, 0, 101), -0.5, None, A.add, off=V("colo", 0, 2))
+            for b in range(nw):
+                diagonal(b)
+            for b in range(nw):
+                magnitudes(b)
+                raise_diagonal(b)
+            for b in range(nw):
+                diagonal_sum(b)
+        else:
+            for b in range(nw):
+                magnitudes(b)
+            diagonal(0)
+            diagonal(1)
 
-        for s in range(S):
+        for s in range(z, S):
             if s:
                 o0 = 10 * ((s - 1) // 2) + 6 * ((s - 1) % 2)
                 cp(V("gt", 0, 16 * nw), V("ga", 0, nw * n), off=V(off, o0, o0 + nw))
@@ -358,25 +412,45 @@ def rank_program(g, core, T, topo):
                         mm(4, P, nx, 0, "m0")
                         dma("y", T.oc[:, 0:256], V(nx + "q", 0, 64))
                     elif i == 0:
+                        send(peer, [(V(nx + "q", 96, 128), V(nx + "q", 192, 224))], ab)
+                        send(peer, [(V(nx + "s", 96, 128), V(nx + "s", 192, 224))], ab)
+                        repeat(nx, 160, 192, "dc%d" % (c + 1))
+                        repeat(nx, 128, 192, "dd%d" % (c + 1))
                         repeat(nx, 224, 192, "da%d" % (c + 1))
-                        send(peer, [(V(nx + "s", 96, 128), V(nx + "s", 192, 224))], ar)
                     else:
                         repeat(nx, 0, 160, "db%d" % (c + 1))
-                        send(peer, [(V(nx + "q", 64, 128), V(nx + "q", 160, 224))], ar)
+                        send(peer, [(V(nx + "q", 64, 96), V(nx + "q", 160, 192))], ar)
                 elif s == 5 and not last:
                     pick(nx, 128, m, m0, n, V(off, 24, 25))
                     send(peer, [(V(nx + "q", 32, 48), V(nx + "q", 128, 144))], ar)
+                elif s == 1 and c:
+                    for b in range(nw):
+                        raise_diagonal(b)
+                    diagonal(2)
+                    cp(V(tn, 96, 98), V("ln%d" % c, 0, 2))
                 else:
                     between()
                 scan(V("sc", 0, 16 * nw), V("keep", 0, 16 * nw), V("gt", 0, 16 * nw), A.mult, A.max)
-                between()
+                if s == 1 and c:
+                    for b in range(nw):
+                        diagonal_sum(b)
+                    for b in range(2):
+                        ts(V("pn", 32 * b, 32 * b + 32), V("zero", 0, 32), V(tn, 96 + b, 97 + b), None, A.add)
+                    ts(V("ncol", 0, 32), V(tn, 0, 99), -0.5, None, A.add, off=V("colo", 0, 2))
+                else:
+                    between()
             for b in range(nw):
-                blk = V("nb", 32 * b, 32 * b + 32)
-                ts(blk, blk if s else V("zero", 0, 32), V("sc", 16 * b + 15, 16 * b + 16), None, A.add)
-            if s == 0 and c:
-                tp(V(nat, 0, 32), V("pn", 0, 32))
-                signs(c)
-            elif s == 0:
+                blk, drop = V("nb", 32 * b, 32 * b + 32), V("sc", 16 * b + 15, 16 * b + 16)
+                if s > z:
+                    ts(blk, blk, drop, None, A.add)
+                elif z:
+                    if b == 0:
+                        tp(V(nat, 0, 64), V("pn", 0, 64))
+                        signs(c)
+                    ts(blk, blk, V("dg", b, b + 1), drop, A.add, A.add)
+                else:
+                    ts(blk, V("zero", 0, 32), V("dg", b, b + 1), None, A.add)
+            if s == 0:
                 multipliers(0, 1)
             else:
                 between()
@@ -391,11 +465,9 @@ def rank_program(g, core, T, topo):
                 for a in range(2):
                     e0 = a * (n + 2) + part * H
                     ts(V("eq" + t, e0, e0 + H), V("nr", part * H, part * H + H), col[a], None, A.is_equal)
-            if s == 0 and c:
+            if s == 1 and c:
                 multipliers(c, 0)
                 multipliers(c, 1)
-            else:
-                between()
             for a in range(2):
                 e0 = a * (n + 2)
                 scan(V("eo", e0, e0 + n + 1), V("sig", e0, e0 + n + 1), V("eq" + t, e0, e0 + n + 1), A.mult, A.add)
@@ -404,24 +476,26 @@ def rank_program(g, core, T, topo):
             if s == 4 and last:
                 ac(V("zsb", 0, P, 0, 64), V("ps", 2048, 2048 + P, 0, 64), F.Copy)
                 dma("y", T.z[0:64, :], V("zsb", 0, P, 0, 64))
-            if s == 4 and not last:
-                tp(V(tnx, 32, 96), V(natx, 128, 192))
-            else:
-                between()
             for a in range(2):
                 e1 = a * (n + 2) + n
                 for p0, p1, d0, c0 in ((0, 96, 0, 32 * a), (96, 128, 32 * a, 64))[:2 - z]:
                     ts(V("pre", c0, c0 + 32, d0, d0 + p1 - p0), V("ks", 32 * a, 32 * a + 32, p0, p1),
                        V("eo", e1, e1 + 1, p0, p1), V("pb" + t, ranked[a], ranked[a] + 1, p0, p1), A.is_equal, A.mult)
-            if s == 4 and not last:
-                cp(V("sn%d" % (c + 1), 0, 2), V(tnx, 32, 96, step=32))
-                send(peer, [(V("ln%d" % (c + 1), 0, 2), V("sn%d" % (c + 1), 0, 2))], "ae%d" % (c + 1))
+            if s == 2 and not last:
+                tp(V(tnx, 64, 96), V(natx, 160, 192))
             else:
                 between()
             tp(V("tr" + t, 0, tail, 0, 96), V("pre", 0, tail, 0, 96))
-            between()
+            if s == 2 and not last:
+                cp(V("sa%d" % (c + 1), 0, 2), V(tnx, 64, 66))
+                send(peer, [(V("la%d" % (c + 1), 0, 2), V("sa%d" % (c + 1), 0, 2))], "ae%d" % (c + 1))
+            else:
+                between()
             scan(V("to", 0, tail + 6, 0, 96), V("zero", 0, tail + 6, 0, 96), V("tr" + t, 0, tail + 6, 0, 96), A.add, A.add)
             between()
+            if s == 3 and not last:
+                mm(5, 128, nx, 96, nx, 96)
+                spare.extend(first_step(c + 1))
             o0, b0 = 10 * (s // 2) + 5 * (s % 2), tail + 1 - s % 2
             for q in range(4):
                 ts(V(off, o0, o0 + 5, 32 * q, 32 * q + 32), V("to", b0, b0 + 5, 0, 32),
@@ -434,10 +508,15 @@ def rank_program(g, core, T, topo):
         pick(nx, 144, m, m0, n, V(off, 26, 27))
         send(peer, [(V(nx + "q", 48, 64), V(nx + "q", 144, 160)), (V(nx + "s", 32, 96), V(nx + "s", 128, 192))], ar)
         cp(V(natx, 96, 128), V(nat, 0, n), off=pair[2])
-        tp(V(tnx, 0, 32), V(natx, 96, 128))
-        send(peer, [(V(tnx, 100, 101), V(tnx, 0, 1))], "an%d" % (c + 1))
+        between()
+        tp(V(tnx, 0, 64), V(natx, 96, 160))
+        between()
+        cp(V("sn%d" % (c + 1), 0, 2), V(tnx, 0, 64, step=32))
+        send(peer, [(V("ln%d" % (c + 1), 0, 2), V("sn%d" % (c + 1), 0, 2))], "an%d" % (c + 1))
         while spare:
             between()
+        if c == 1:
+            quant("w", "wt", 0, 128 * O)
 
     for c in range(3):
         choice(c)

@@ -4,6 +4,7 @@ from concourse.mybir import dt, AluOpType as A, AxisListType, ActivationFunction
 P, K, S, O = 256, 16, 6, 3
 W = K * S
 BIG = 1e29
+LOW = -9e29
 Q4, U8, F32, BF, U16, I32 = "float8_e4m3fn_x4", "uint8", "float32", "bfloat16", "uint16", "int32"
 
 
@@ -17,7 +18,7 @@ SCRATCH = {
     "m1q": _sb(256, Q4), "m1s": _sb(256, U8), "m2q": _sb(256, Q4), "m2s": _sb(256, U8),
     "m3q": _sb(128, Q4), "m3s": _sb(128, U8),
     "ps": ("psum", [128, 4096], F32),
-    "ga": _sb(1024, F32), "nb": _sb(128, F32), "nr": _sb(256, F32), "gt": _sb(64, F32), "sc": _sb(64, F32),
+    "ga": _sb(1024, F32), "nb": _sb(192, F32), "gh": _sb(192, F32), "nr": _sb(256, F32), "gt": _sb(64, F32), "sc": _sb(64, F32),
     "dgo": _sb(512, F32), "dg": _sb(4, F32), "keep": _sb(64, F32), "negi": _sb(128, F32),
     "j16": _sb(64, F32), "zero": _sb(104, F32),
     "eq0": _sb(516, BF), "eq1": _sb(388, BF), "tau0": _sb(516, BF), "tau1": _sb(388, BF),
@@ -47,6 +48,11 @@ def V(name, c0, c1, p0=0, p1=128, step=1):
     return (name, p0, p1, c0, c1, step)
 
 
+def block(b):
+    c = 96 * (b // 2) + 16 + 32 * (b % 2)
+    return V("nb", c, c + 32)
+
+
 def rank_program(g, core, T, topo):
     rank = T.rank_of(core)
     if rank is None:
@@ -58,6 +64,8 @@ def rank_program(g, core, T, topo):
     seen = {}
 
     def ap(v):
+        if v[5] == -1:
+            return T[v[0]][v[1]:v[2], v[4] - 1:(v[3] - 1 if v[3] else None):-1]
         return T[v[0]][v[1]:v[2], v[3]:v[4]:v[5]] if v[5] != 1 else T[v[0]][v[1]:v[2], v[3]:v[4]]
 
     def box(v):
@@ -77,7 +85,7 @@ def rank_program(g, core, T, topo):
     def note(v, writes, q, h):
         b = box(v)
         old = seen.get(v[0], [])
-        if writes and v[5] == 1:
+        if writes and v[5] in (1, -1):
             old = [e for e in old if not (b[0] <= e[0] and e[1] <= b[1] and b[2] <= e[2] and e[3] <= b[3])]
         seen[v[0]] = old + [b + (writes, q, h)]
 
@@ -120,8 +128,9 @@ def rank_program(g, core, T, topo):
             return op("v", lambda: vec.tensor_scalar(ap(out), a0, a1, None, op0), rd, [out])
         return op("v", lambda: vec.tensor_scalar(ap(out), a0, a1, a2, op0, op1), rd, [out])
 
-    def tt(out, in0, in1, o):
-        return op("v", lambda: vec.tensor_tensor(ap(out), ap(in0), ap(in1), o), [in0, in1], [out])
+    def tt(out, in0, in1, o, off=None):
+        a0 = ap(in0) if off is None else ap(in0).indirect(ap(off))
+        return op("v", lambda: vec.tensor_tensor(ap(out), a0, ap(in1), o), [a for a in (in0, in1, off) if a], [out])
 
     def cp(out, in0, off=None):
         a0 = ap(in0) if off is None else ap(in0).indirect(ap(off))
@@ -133,8 +142,8 @@ def rank_program(g, core, T, topo):
     def tp(out, in0):
         return op("v", lambda: vec.transpose(ap(out), ap(in0)), [in0], [out])
 
-    def scan(out, d0, d1, o0, o1):
-        return op("v", lambda: vec.tensor_tensor_scan(ap(out), ap(d0), ap(d1), 0.0, o0, o1), [d0, d1], [out])
+    def scan(out, d0, d1, o0, o1, init=0.0):
+        return op("v", lambda: vec.tensor_tensor_scan(ap(out), ap(d0), ap(d1), init, o0, o1), [d0, d1], [out])
 
     def total(out, in0):
         return op("v", lambda: vec.tensor_reduce(ap(out), ap(in0), AxisListType.X, A.add), [in0], [out])
@@ -233,6 +242,7 @@ def rank_program(g, core, T, topo):
     iota(V("cb0", 0, 6), [[256, 6]], -256, 0)
     iota(V("pos1", 0, 4), [[128, 2], [32, 2]], -32, 1)
     iota(V("cb1", 0, 6), [[192, 6]], -192, 0)
+    ms(V("gh", 0, 192), LOW)
     ts(V("ii", 0, 1), V("ii", 0, 1), 31, None, A.bitwise_and)
     ts(V("ii", 1, 2), V("ii", 1, 2), 15, None, A.bitwise_and)
     ms(V("zero", 0, 104), 0.0)
@@ -343,8 +353,9 @@ def rank_program(g, core, T, topo):
         place = (0, 32, 64) if last else (192, 160, 128)
         placen = place if last else (160, 128, 96)
         pair = [V(off, 10 * i + 4, 10 * i + 6) for i in range(3)]
-        col = [V("nb", 32 * b, 32 * b + 1) for b in ranked]
+        col = [V("nb", block(b)[3], block(b)[3] + 1) for b in ranked]
         peer, ar, ab = peers.get(c + 1), "ar%d" % (c + 1), "ab%d" % (c + 1)
+        held = (2, nw - 2)
 
         def runs(b):
             st, q, out = starts[b], 0, []
@@ -372,6 +383,12 @@ def rank_program(g, core, T, topo):
         def diagonal_sum(b):
             total(V("dg", b, b + 1), V("dgo", 128 * b, 128 * b + 128))
 
+        def turn(i, k):
+            w = 32 * held[i]
+            po, pi = ((0, 128), (0, 64), (64, 128))[k], ((0, 128), (64, 128), (0, 64))[k]
+            d = 64 * i + (H if k else 0)
+            tp(V("nr", d, d + w, *po), V("nb", 96 * i + 16, 96 * i + 16 + w, *pi))
+
         if c:
             tn = "tn%d" % c
             ts(V("lr", 0, 16), V("nat0", 0, n), -float(P * rank), None, A.add, off=V(off, 0, 1))
@@ -379,7 +396,7 @@ def rank_program(g, core, T, topo):
                 ts(V("gt", 16 * b, 16 * b + 16), V("lr", 0, 16), V("pos1", b, b + 1), BIG, A.is_equal, A.mult)
             scan(V("sc", 0, 16 * nw), V("keep", 0, 16 * nw), V("gt", 0, 16 * nw), A.mult, A.max)
             for b in range(nw):
-                ts(V("nb", 32 * b, 32 * b + 32), V("zero", 0, 32), V("sc", 16 * b + 15, 16 * b + 16), None, A.add)
+                ts(block(b), V("zero", 0, 32), V("sc", 16 * b + 15, 16 * b + 16), None, A.add)
         for b in range(nw):
             mm(b, n, m, 32 * starts[b], m, m0)
         if c == 0:
@@ -400,7 +417,13 @@ def rank_program(g, core, T, topo):
         for s in range(z, S):
             if s:
                 o0 = 10 * ((s - 1) // 2) + 6 * ((s - 1) % 2)
-                cp(V("gt", 0, 16 * nw), V("ga", 0, nw * n), off=V(off, o0, o0 + nw))
+                if s > z:
+                    for i in range(2):
+                        c0, k = 96 * i + 32, held[i]
+                        tt(V("gh", c0, c0 + 16 * k), V("ga", 0, nw * n), V("nb", c0, c0 + 16 * k), A.add,
+                           off=V(off, o0 + 2 * i, o0 + 2 * i + k))
+                else:
+                    cp(V("gt", 0, 16 * nw), V("ga", 0, nw * n), off=V(off, o0, o0 + nw))
                 if s in (2, 4):
                     i = s // 2 - 1
                     pick(nx, place[i], m, m0, n, pair[i])
@@ -430,33 +453,30 @@ def rank_program(g, core, T, topo):
                     cp(V(tn, 96, 98), V("ln%d" % c, 0, 2))
                 else:
                     between()
+            if s > z:
+                for b in range(nw):
+                    c0, way = 96 * (b // 2) + 48 * (b % 2), 1 - 2 * (b % 2)
+                    scan(V("nb", c0, c0 + 48, step=way), V("zero", 0, 48), V("gh", c0, c0 + 48, step=-way), A.add, A.max, LOW)
+            elif z:
                 scan(V("sc", 0, 16 * nw), V("keep", 0, 16 * nw), V("gt", 0, 16 * nw), A.mult, A.max)
-                if s == 1 and c:
-                    for b in range(nw):
-                        diagonal_sum(b)
-                    for b in range(2):
-                        ts(V("pn", 32 * b, 32 * b + 32), V("zero", 0, 32), V(tn, 96 + b, 97 + b), None, A.add)
-                    ts(V("ncol", 0, 32), V(tn, 0, 99), -0.5, None, A.add, off=V("colo", 0, 2))
-                else:
-                    between()
-            for b in range(nw):
-                blk, drop = V("nb", 32 * b, 32 * b + 32), V("sc", 16 * b + 15, 16 * b + 16)
-                if s > z:
-                    ts(blk, blk, drop, None, A.add)
-                elif z:
-                    if b == 0:
-                        tp(V(nat, 0, 64), V("pn", 0, 64))
-                        signs(c)
-                    ts(blk, blk, V("dg", b, b + 1), drop, A.add, A.add)
-                else:
-                    ts(blk, V("zero", 0, 32), V("dg", b, b + 1), None, A.add)
+                for b in range(nw):
+                    diagonal_sum(b)
+                for b in range(2):
+                    ts(V("pn", 32 * b, 32 * b + 32), V("zero", 0, 32), V(tn, 96 + b, 97 + b), None, A.add)
+                ts(V("ncol", 0, 32), V(tn, 0, 99), -0.5, None, A.add, off=V("colo", 0, 2))
+                tp(V(nat, 0, 64), V("pn", 0, 64))
+                signs(c)
+                for b in range(nw):
+                    ts(block(b), block(b), V("dg", b, b + 1), V("sc", 16 * b + 15, 16 * b + 16), A.add, A.add)
+            else:
+                for b in range(nw):
+                    ts(block(b), V("zero", 0, 32), V("dg", b, b + 1), None, A.add)
             if s == 0:
                 multipliers(0, 1)
             else:
                 between()
-            tp(V("nr", 0, H), V("nb", 0, H))
-            tp(V("nr", H, n, 0, 64), V("nb", 0, H, 64, 128))
-            tp(V("nr", H, n, 64, 128), V("nb", 0, H, 0, 64))
+            for i, k in (((0, 0), (0, 1), (1, 0), (0, 2), (1, 1), (1, 2)), ((0, 0), (1, 0), (0, 1), (0, 2), (1, 1), (1, 2)))[z]:
+                turn(i, k)
             for part in range(2):
                 for a in range(2):
                     ac(V("junk", 256 * a + part * H, 256 * a + part * H + H), V("nr", part * H, part * H + H), F.Sign,
@@ -468,6 +488,8 @@ def rank_program(g, core, T, topo):
             if s == 1 and c:
                 multipliers(c, 0)
                 multipliers(c, 1)
+            elif s:
+                between()
             for a in range(2):
                 e0 = a * (n + 2)
                 scan(V("eo", e0, e0 + n + 1), V("sig", e0, e0 + n + 1), V("eq" + t, e0, e0 + n + 1), A.mult, A.add)

@@ -6,6 +6,7 @@ W = K * S
 BIG = 1e29
 LOW = -9e29
 Q4, U8, F32, BF, U16, I32 = "float8_e4m3fn_x4", "uint8", "float32", "bfloat16", "uint16", "int32"
+L0, L1, LM = 256 + 33, 192 + 33, 16 + 32
 
 
 def _sb(n, d):
@@ -13,44 +14,49 @@ def _sb(n, d):
 
 
 SCRATCH = {
-    "xt": _sb(4 * (P + 32), BF), "m0q": _sb(P + 32, Q4), "m0s": _sb(P + 32, U8),
+    "xt": _sb(4 * (P + 64), BF), "m0q": _sb(P + 64, Q4), "m0s": _sb(P + 64, U8),
     "wt": _sb(512 * O, BF), "wq": _sb(128 * O, Q4), "ws": _sb(128 * O, U8),
     "m1q": _sb(256, Q4), "m1s": _sb(256, U8), "m2q": _sb(256, Q4), "m2s": _sb(256, U8),
     "m3q": _sb(128, Q4), "m3s": _sb(128, U8),
+    "u1q": _sb(128, Q4), "u1s": _sb(128, U8), "u2q": _sb(128, Q4), "u2s": _sb(128, U8),
     "ps": ("psum", [128, 4096], F32),
-    "ga": _sb(1024, F32), "nb": _sb(192, F32), "gh": _sb(192, F32), "nr": _sb(256, F32), "gt": _sb(64, F32), "sc": _sb(64, F32),
-    "dgo": _sb(512, F32), "dg": _sb(4, F32), "keep": _sb(64, F32), "negi": _sb(128, F32),
-    "j16": _sb(64, F32), "zero": _sb(104, F32),
-    "eq0": _sb(516, BF), "eq1": _sb(388, BF), "tau0": _sb(516, BF), "tau1": _sb(388, BF),
-    "sig": _sb(516, BF), "eo": _sb(516, BF), "junk": _sb(512, BF),
-    "eqm": _sb(66, BF), "taum": _sb(66, BF), "sigm": _sb(66, BF), "kcm": _sb(32, F32), "trm": _sb(40, F32),
-    "pbm": _sb(2, BF), "colm": _sb(2, F32), "dgm": _sb(128, F32), "dm": _sb(1, F32), "pnm": _sb(32, F32),
-    "nbm": _sb(64, F32), "nrm": _sb(64, F32), "junkm": _sb(64, BF), "accm": _sb(1, F32), "eom": _sb(66, BF),
-    "ksm": _sb(32, F32), "prem": _sb(32, F32), "tom": _sb(40, F32), "lr": _sb(16, F32),
-    "acc": _sb(4, F32), "ks": _sb(64, F32), "pre": _sb(96, F32), "to": _sb(104, F32),
-    "tr0": _sb(104, F32), "tr1": _sb(72, F32), "ii": _sb(2, I32), "pf": _sb(2, F32), "pr": _sb(1, F32),
-    "kc0": _sb(32, F32), "kc1": _sb(32, F32), "cb0": _sb(6, F32), "cb1": _sb(6, F32),
-    "pos0": _sb(4, F32), "pos1": _sb(4, F32), "pb0": _sb(4, BF), "pb1": _sb(4, BF),
-    "tmp0": _sb(16, F32), "tmp1": _sb(16, F32), "blk0": _sb(8, F32), "blk1": _sb(8, F32),
-    "perm0": _sb(16, U16), "perm1": _sb(12, U16), "colo": _sb(2, U16),
-    "off0": _sb(30, U16), "off1": _sb(30, U16), "off2": _sb(30, U16),
+    "ga": _sb(1024, F32), "nb": _sb(640, F32), "gh": _sb(192, F32), "nr": _sb(256, F32),
+    "dgo": _sb(640, F32), "dgy": _sb(128, F32), "dga": _sb(64, F32), "dy": _sb(4, F32), "negi": _sb(128, F32),
+    "zero": _sb(160, F32), "fl": _sb(1, F32),
+    "eq0": _sb(2 * L0, BF), "eq1": _sb(2 * L1, BF), "sig0": _sb(2 * L0, BF), "sig1": _sb(2 * L1, BF),
+    "tau0": _sb(264, BF), "tau1": _sb(296, BF), "eo": _sb(2 * L0, BF), "junk": _sb(512, BF),
+    "tr0": _sb(130, BF), "tr1": _sb(64, BF), "am": _sb(1, F32), "acc": _sb(2, F32), "cb0": _sb(4, F32),
+    "dgm": _sb(64, F32), "nbm": _sb(64, F32), "nrm": _sb(32, F32), "eqm": _sb(LM, BF), "sigm": _sb(LM, BF),
+    "eom": _sb(LM, BF), "trm": _sb(34, BF), "amm": _sb(1, F32), "idm": _sb(1, F32), "cbm": _sb(3, F32),
+    "ii": _sb(2, I32), "pf": _sb(2, F32), "pr": _sb(1, F32),
+    "pos0": _sb(4, F32), "pos1": _sb(4, F32), "blk0": _sb(8, F32), "blk1": _sb(8, F32),
+    "perm0": _sb(16, U16), "perm1": _sb(16, U16),
+    "off0": _sb(24, U16), "off1": _sb(14, U16), "off2": _sb(14, U16),
     "nat0": _sb(256, F32), "nat1": _sb(192, F32), "nat2": _sb(192, F32), "nat3": _sb(96, F32),
-    "tn1": _sb(104, F32), "tn2": _sb(104, F32), "pn": _sb(64, F32), "ncol": _sb(32, F32),
-    "sn1": _sb(2, U16), "sn2": _sb(2, U16), "ln1": _sb(2, U16), "ln2": _sb(2, U16),
-    "sa1": _sb(2, U16), "sa2": _sb(2, U16), "la1": _sb(2, U16), "la2": _sb(2, U16),
-    "ysb": _sb(O * W, F32), "zsb": _sb(P, F32),
+    "tn1": _sb(96, F32), "tn2": _sb(96, F32), "pn": _sb(96, F32), "ncol": _sb(2, F32), "lf": _sb(2, F32),
+    "ln1": _sb(1, F32), "ln2": _sb(1, F32), "sa1": _sb(2, U16), "sa2": _sb(2, U16), "la1": _sb(2, U16), "la2": _sb(2, U16),
+    "yall": _sb(O * 192, F32), "ysb": _sb(O * W, F32), "zsb": _sb(P, F32),
 }
-SEMAPHORES = ["cv", "cs", "ct", "cg", "lx", "lw", "ar1", "ar2", "ab1", "ab2", "an1", "an2", "ae1", "ae2", "sent",
-              "da1", "db1", "dc1", "dd1", "da2", "db2", "dc2", "dd2", "da3", "db3", "st"]
+SEMAPHORES = ["cv", "cs", "ct", "cg", "lxa", "lxb", "lw", "ar1", "ar2", "ab1", "ab2", "an1", "an2", "ae1", "ae2", "sent",
+              "da1", "db1", "dc1", "dd1", "da2", "db2", "dc2", "dd2", "da3", "db3", "du1", "du2", "st"]
 
 
 def V(name, c0, c1, p0=0, p1=128, step=1):
     return (name, p0, p1, c0, c1, step)
 
 
-def block(b):
-    c = 96 * (b // 2) + 16 + 32 * (b % 2)
-    return V("nb", c, c + 32)
+def at(b):
+    return 320 * (b // 2) + 128 + 32 * (b % 2)
+
+
+def block(b, p0=0, p1=128):
+    return V("nb", at(b), at(b) + 32, p0, p1)
+
+
+def into(b, lead, p0=0, p1=128):
+    if b % 2 == 0:
+        return V("nb", at(b) - lead, at(b) + 32, p0, p1)
+    return V("nb", at(b), at(b) + 32 + lead, p0, p1, -1)
 
 
 def rank_program(g, core, T, topo):
@@ -120,13 +126,12 @@ def rank_program(g, core, T, topo):
     def isv(a):
         return isinstance(a, tuple)
 
-    def ts(out, in0, s1, s2, op0, op1=None, off=None):
-        rd = [a for a in (in0, s1, s2, off) if isv(a)]
-        a0 = ap(in0) if off is None else ap(in0).indirect(ap(off))
+    def ts(out, in0, s1, s2, op0, op1=None):
+        rd = [a for a in (in0, s1, s2) if isv(a)]
         a1, a2 = (ap(s1) if isv(s1) else s1), (ap(s2) if isv(s2) else s2)
         if op1 is None:
-            return op("v", lambda: vec.tensor_scalar(ap(out), a0, a1, None, op0), rd, [out])
-        return op("v", lambda: vec.tensor_scalar(ap(out), a0, a1, a2, op0, op1), rd, [out])
+            return op("v", lambda: vec.tensor_scalar(ap(out), ap(in0), a1, None, op0), rd, [out])
+        return op("v", lambda: vec.tensor_scalar(ap(out), ap(in0), a1, a2, op0, op1), rd, [out])
 
     def tt(out, in0, in1, o, off=None):
         a0 = ap(in0) if off is None else ap(in0).indirect(ap(off))
@@ -143,10 +148,12 @@ def rank_program(g, core, T, topo):
         return op("v", lambda: vec.transpose(ap(out), ap(in0)), [in0], [out])
 
     def scan(out, d0, d1, o0, o1, init=0.0):
-        return op("v", lambda: vec.tensor_tensor_scan(ap(out), ap(d0), ap(d1), init, o0, o1), [d0, d1], [out])
+        a = ap(init) if isv(init) else init
+        return op("v", lambda: vec.tensor_tensor_scan(ap(out), ap(d0), ap(d1), a, o0, o1),
+                  [d0, d1] + [init] * isv(init), [out])
 
-    def total(out, in0):
-        return op("v", lambda: vec.tensor_reduce(ap(out), ap(in0), AxisListType.X, A.add), [in0], [out])
+    def red(out, in0, o, size=False):
+        return op("v", lambda: vec.tensor_reduce(ap(out), ap(in0), AxisListType.X, o, apply_absolute_value=size), [in0], [out])
 
     def quant(m, src, c0, c1):
         o, s, i = V(m + "q", c0, c1), V(m + "s", c0, c1), V(src, 4 * c0, 4 * c1)
@@ -173,11 +180,13 @@ def rank_program(g, core, T, topo):
         return op("t", lambda: g.tensor.matmul_mx(ap(out), ap(a[0]), ap(a[1]), ap(b[0]), ap(b[1]), True, True),
                   list(a + b), [out])
 
+    def bank(b, c0, c1, p0=0, p1=128):
+        return V("ps", 512 * b + c0, 512 * b + c1, p0, p1)
+
     def pick(dst, d0, src, s0, n, off):
-        k = 16 * (off[4] - off[3])
-        o, i = V(dst + "q", d0, d0 + k), V(src + "q", s0, s0 + n)
+        o, i = V(dst + "q", d0, d0 + 16), V(src + "q", s0, s0 + n)
         op("v", lambda: vec.tensor_copy(ap(o).bitcast(dt.uint32), ap(i).bitcast(dt.uint32).indirect(ap(off))), [i, off], [o])
-        ac(V(dst + "s", d0, d0 + k), V(src + "s", s0, s0 + n), F.Copy, off=off)
+        ac(V(dst + "s", d0, d0 + 16), V(src + "s", s0, s0 + n), F.Copy, off=off)
 
     def raw(v):
         return ap(v).bitcast(dt.uint8) if SCRATCH[v[0]][2] == Q4 else ap(v)
@@ -185,10 +194,10 @@ def rank_program(g, core, T, topo):
     def dma(q, out, v):
         return op(q, lambda: queue[q].dma_start(out, raw(v)), [v], [], sem="st", inc=16)
 
-    def repeat(m, d0, s0, sem):
+    def repeat(m, d0, s0, sem, src=None, k=32):
         hs = []
         for e in "qs":
-            o, i = V(m + e, d0, d0 + 32), V(m + e, s0, s0 + 32)
+            o, i = V(m + e, d0, d0 + k), V((src or m) + e, s0, s0 + k)
             order("y", [i], [o])
             g.sync.dma_start(raw(o), raw(i)).then_inc(T.sem[sem], 16)
             hs.append((o, i))
@@ -215,6 +224,10 @@ def rank_program(g, core, T, topo):
                                 for i, (d, s) in enumerate(pieces)], local_sem=T.sem.sent)
         sent[0] += len(es)
 
+    def run(calls):
+        for call in calls:
+            call[0](*call[1:])
+
     peers = {c: T.cores[rank ^ (1 << (c - 1))] for c in (1, 2)}
     for c in (1, 2):
         ne = len(topo.engines(peers[c], core))
@@ -222,323 +235,367 @@ def rank_program(g, core, T, topo):
             note(V("m%d%s" % (c, e), 32, 96), True, None, ("ar%d" % c, 3 * ne, {}))
             note(V("m%d%s" % (c, e), 96, 128), True, None, ("ab%d" % c, 2 * ne, {}))
         note(V("la%d" % c, 0, 2), True, None, ("ae%d" % c, ne, {}))
-        note(V("ln%d" % c, 0, 2), True, None, ("an%d" % c, ne, {}))
+        note(V("ln%d" % c, 0, 1), True, None, ("an%d" % c, ne, {}))
 
-    shape = {0: (256, (0, 1, 4, 5), (0, 1, 2, 3, 4, 5, 6, 7, 0), 0, (0, 2)),
-             1: (192, (0, 1, 4), (4, 0, 1, 2, 3, 4, 5, 5), 1, (1, 2))}
+    shape = {0: (256, (0, 1, 5, 6), (3, 0, 1, 2, 3, 4, 5, 6, 7, 4), (1, 2), ((0, 128), (128, 256))),
+             1: (192, (1, 0, 4), (4, 0, 1, 2, 3, 4, 5, 5), (0, 2), ((0, 128), (32, 192)))}
 
-    hx = ("lx", 32, {})
-    g.sync.dma_start(ap(V("xt", 0, 4 * P)), T.x[:]).then_inc(T.sem.lx, 16)
-    g.scalar.dma_start(ap(V("xt", 4 * P, 4 * P + 128)), T.x[:, 0:128]).then_inc(T.sem.lx, 16)
-    note(V("xt", 0, 4 * P + 128), True, "y", hx)
-    wait("y", hx)
+    for sem, h in (("lxa", 0), ("lxb", 1)):
+        g.sync.dma_start(ap(V("xt", 128 + 512 * h, 640 + 512 * h)), T.x[:, 512 * h:512 * h + 512]).then_inc(T.sem[sem], 16)
+        g.scalar.dma_start(ap(V("xt", 1152 * h, 1152 * h + 128)), T.x[:, 384 + 128 * h:512 + 128 * h]).then_inc(T.sem[sem], 16)
+        note(V("xt", 640 * h, 640 * h + 640), True, "y", (sem, 32, {}))
+    wait("y", ("lxb", 32, {}))
     op("y", lambda: g.sync.dma_start(T.wt[:], T.w[:]), [], [V("wt", 0, 512 * O)], sem="lw", inc=16)
 
     iota(V("ii", 0, 2), [[0, 2]], 0, 1)
     iota(V("pos0", 0, 4), [[128, 2], [32, 2]], 0, 1)
     iota(V("nat0", 0, 256), [[1, 256]], P * rank, 0)
     iota(V("pr", 0, 1), [[0, 1]], P * rank, 1)
-    iota(V("j16", 0, 64), [[0, 4], [1, 16]], 0, 0)
-    iota(V("cb0", 0, 6), [[256, 6]], -256, 0)
-    iota(V("pos1", 0, 4), [[128, 2], [32, 2]], -32, 1)
-    iota(V("cb1", 0, 6), [[192, 6]], -192, 0)
-    ms(V("gh", 0, 192), LOW)
-    ts(V("ii", 0, 1), V("ii", 0, 1), 31, None, A.bitwise_and)
-    ts(V("ii", 1, 2), V("ii", 1, 2), 15, None, A.bitwise_and)
-    ms(V("zero", 0, 104), 0.0)
-    ms(V("pre", 64, 96), 0.0)
-    ts(V("ncol", 0, 17, step=16), V("pos0", 0, 3, step=2), P * rank - 0.5, None, A.add)
-    cp(V("pf", 0, 2), V("ii", 0, 2))
+    iota(V("cb0", 0, 4), [[256, 4]], -256, 0)
+    iota(V("pos1", 0, 4), [[96, 2], [-32, 2]], 0, 1)
+    iota(V("cbm", 0, 3), [[32, 3]], -320, 0)
+
+    def tail(e, c0, down):
+        d = 512.0 if down else -512.0
+        return [(ms, V(e, c0 + 1, c0 + 32), d), (ms, V(e, c0 + 16, c0 + 17), -15 * d)]
 
     def tables(z):
-        n, starts, seq, first, ranked = shape[z]
-        nw, t, tail = len(starts), str(z), (96, 64)[z]
+        n, starts, seq, ranked, part = shape[z]
+        nw, t, L = len(starts), str(z), n + 33
+        k1 = nw - 2
+        m = [hi - lo for lo, hi in part]
         calls = []
         for b, st in enumerate(starts):
             for q in range(4):
-                if seq[st + q] != st + q - first:
+                if seq[st + q] != st + q - 1:
                     v = V("pos" + t, b, b + 1, 32 * q, 32 * q + 32)
-                    calls.append((ts, v, v, float(32 * (seq[st + q] - st - q + first)), None, A.add))
-        calls += [
-            (ms, V("tau" + t, 0, n + 3, step=n + 2), 0.0),
-            (ms, V("eq" + t, n, n + 2), 0.0),
-            (ms, V("eq" + t, 2 * n + 2, 2 * n + 4), 0.0),
-            (ts, V("blk" + t, 0, nw), V("pos" + t, 0, nw), V("pf", 0, 1), None, A.subtract),
-            (ms, V("tau" + t, n + 1, 2 * n + 4, step=n + 2), 1.0),
-            (cp, V("pb" + t, 0, nw), V("pos" + t, 0, nw)),
-            (ms, V("tr" + t, tail, tail + 1), 0.0),
-            (cp, V("blk" + t, nw, 2 * nw, 0, 64), V("blk" + t, 0, nw, 64, 128)),
-            (cp, V("blk" + t, nw, 2 * nw, 64, 128), V("blk" + t, 0, nw, 0, 64)),
-            (ms, V("cb" + t, 0, 6, step=5), 0.0),
-            (ts, V("kc" + t, 0, 32), V("j16", 0, 32), 2.0, float(-n), A.mult, A.add),
-            (ts, V("tmp" + t, 0, 2 * nw), V("blk" + t, 0, 2 * nw), V("pf", 1, 2), None, A.add),
-            (tt, V("tr" + t, tail + 1, tail + 6), V("cb" + t, 1, 6), V("cb" + t, 0, 5), A.subtract),
-            (cp, V("perm" + t, 0, 4 * nw, step=2), V("tmp" + t, 0, 2 * nw)),
-            (ts, V("kcm", 0, 32), V("j16", 0, 32), 2.0, -64.0, A.mult, A.add) if z else (ms, V("taum", 0, 1), 0.0),
-            (ts, V("perm" + t, 1, 4 * nw, step=2), V("tmp" + t, 0, 2 * nw), 16.0, None, A.add)]
+                    calls.append((ts, v, v, float(32 * (seq[st + q] - st - q + 1)), None, A.add))
+        calls += [(ms, V("sig" + t, 0, 2 * L), 1.0),
+                  (ms, V("tau" + t, 0, 1), 1.0), (ms, V("tau" + t, m[0] + 1, m[0] + 2), 0.5),
+                  (ms, V("tau" + t, m[0] + 2, m[0] + 3), 2.0), (ms, V("tau" + t, m[0] + m[1] + 3, m[0] + m[1] + 4), 1.0),
+                  (ts, V("blk" + t, 0, 2), V("pos" + t, 0, 2), V("pf", 0, 1), V("pf", 1, 2), A.subtract, A.add),
+                  (ts, V("blk" + t, 4, 4 + k1), V("pos" + t, 2, 2 + k1), V("pf", 0, 1), V("pf", 1, 2), A.subtract, A.add),
+                  (ms, V("sig" + t, n + 1, n + 2), 512.0), (ms, V("sig" + t, L, L + 1), 0.5),
+                  (ms, V("sig" + t, L + n + 1, L + n + 2), 256.0)]
+        for c0, k in ((0, 2), (4, k1)):
+            calls += [(cp, V("blk" + t, c0 + k, c0 + 2 * k, 0, 64), V("blk" + t, c0, c0 + k, 64, 128)),
+                      (cp, V("blk" + t, c0 + k, c0 + 2 * k, 64, 128), V("blk" + t, c0, c0 + k, 0, 64))]
+        calls += [(ms, V("eq" + t, n, n + 1), m[0] / 2.0), (ms, V("eq" + t, L + n, L + n + 1), m[1] - 30.0)]
+        calls += [(cp, V("perm" + t, 0, 4 * nw, step=2), V("blk" + t, 0, 2 * nw)),
+                  (ts, V("perm" + t, 1, 4 * nw, step=2), V("blk" + t, 0, 2 * nw), 16.0, None, A.add)]
+        for a in range(2):
+            calls += tail("eq" + t, a * L + n + 1, a)
+            calls.append((cp, V("eq" + t, a * L + n + 1, a * L + n + 2), V("pos" + t, ranked[a], ranked[a] + 1)))
         return calls
 
-    def signs(c):
+    def signs(c, a):
         z = min(c, 1)
-        n = shape[z][0]
-        for a in range(2):
-            ac(V("tau%d" % z, a * (n + 2) + 1, a * (n + 2) + 1 + n), V("nat%d" % c, 0, n), F.Sign,
-               off=V("perm%d" % z, 0, n // 16), bias=V("ncol", 16 * a, 16 * a + 1))
+        n, part = shape[z][0], shape[z][4]
+        lo, hi = part[a]
+        e0 = 1 + a * (part[0][1] + 2)
+        ac(V("tau%d" % z, e0, e0 + hi - lo), V("nat%d" % c, 0, n), F.Sign,
+           off=V("perm%d" % z, lo // 16, hi // 16), bias=V("ncol", a, a + 1))
 
     def multipliers(c, a):
         z = min(c, 1)
-        n = shape[z][0]
-        e0 = a * (n + 2)
-        tt(V("sig", e0, e0 + n + 1), V("tau%d" % z, e0, e0 + n + 1), V("tau%d" % z, e0 + 1, e0 + n + 2), A.mult)
+        n, part = shape[z][0], shape[z][4]
+        lo, hi = part[a]
+        e0, s0, k = a * (part[0][1] + 2), a * (n + 33) + lo, hi - lo + 1
+        tt(V("sig%d" % z, s0, s0 + k), V("tau%d" % z, e0, e0 + k), V("tau%d" % z, e0 + 1, e0 + k + 1), A.mult)
 
-    for call in tables(0):
-        call[0](*call[1:])
-    signs(0)
+    calls = tables(0)
+    late = [f for f in calls if f[1][0] == "eq0"]
+    late = late[2::3] + late[:2] + late[4::3] + late[3::3]
+    free = [f for f in calls if f[0] is ms and f not in late]
+    free += [(ms, V("dgo", 128, 192), 0.0), (ms, V("dgo", 448, 512), 0.0), (ms, V("tr0", 128, 129), 256.0)]
+    chain = [f for f in calls if f[0] is not ms and f not in late]
+    ms(V("zero", 0, 160), 0.0)
+    run(free[:1])
+    ts(V("ii", 0, 1), V("ii", 0, 1), 31, None, A.bitwise_and)
+    ts(V("ii", 1, 2), V("ii", 1, 2), 15, None, A.bitwise_and)
+    ts(V("pos0", 0, 2), V("pos0", 0, 2), -32.0, None, A.add)
+    run(chain[1:2] + free[1:2])
+    cp(V("pf", 0, 2), V("ii", 0, 2))
+    run(chain[:1] + free[2:5] + chain[2:4])
+    ts(V("ncol", 0, 2), V("pos0", 1, 3), P * rank - 0.5, None, A.add)
+    run(free[5:7] + chain[4:8])
     ts(V("negi", 0, 128), V("nat0", 0, 128), V("pr", 0, 1), -1.0, A.is_equal, A.mult)
-    ts(V("keep", 0, 64), V("j16", 0, 64), 0.0, None, A.is_gt)
-    quant("m0", "xt", 0, P + 32)
+    run(free[7:8] + chain[8:9] + free[8:] + chain[9:])
+    signs(0, 0)
+    signs(0, 1)
 
-    n1, starts1, seq1, first1, ranked1 = shape[1]
-    where = {0: 96, 1: 97, 2: 98, 3: 0, 4: 32, 5: 64}
     early = (64, 160)
     flat = tables(1)
-    for a, b in enumerate(ranked1):
-        for q in range(4):
-            flat.append((ms, V("colo", a, a + 1, 32 * q, 32 * q + 32), where[seq1[starts1[b] + q]]))
-    flat += [(ts, V("pbm", 0, 1, 32 * i, 32 * i + 32), V("pf", 0, 1, 32 * i, 32 * i + 32), float(early[i]), None, A.add)
+    flat += [(ms, V("sigm", 0, LM), 1.0), (ms, V("dgm", 32, 64), 0.0), (ms, V("dga", 32, 64), 0.0), (ms, V("trm", 32, 33), 256.0),
+             (ms, V("fl", 0, 1), 0.0), (ms, V("sigm", 16, 17), 512.0)] + tail("eqm", 16, 0)
+    flat += [(ts, V("eqm", 16, 17, 32 * i, 32 * i + 32), V("pf", 0, 1, 32 * i, 32 * i + 32), float(early[i]), None, A.add)
              for i in range(2)]
-    flat += [(cp, V("trm", 32, 38), V("tr1", 64, 70)), (ms, V("eqm", 64, 66), 0.0), (ms, V("taum", 65, 66), 1.0)]
-    spare = [flat[i:i + 2] for i in range(0, len(flat), 2)]
+    flat += [(ts, V("idm", 0, 1), V("pf", 0, 1), 15.5, 64.0, A.is_gt, A.mult)]
+    flat += [(ts, V("idm", 0, 1), V("idm", 0, 1), V("pf", 0, 1), None, A.add)]
+    for c in (1, 2):
+        flat.append((ms, V("nat%d" % c, 0, 32), -1.0 if rank >> (c - 1) & 1 else 5000.0))
+    fills = [f for f in flat if f[0] is ms and f[2] == int(f[2]) and f[1][4] - f[1][3] <= 64]
+    flat = [f for f in flat if f not in fills]
+    soon, flat = flat[:3], flat[3:]
+    spare = [[(ms, V("gh", 0, 192), LOW)]]
+    spare += [[flat[i] for i in grp] for grp in ((0, 1, 2), (3, 14), (4, 5, 6), (7, 15), (8, 12, 13), (9,), (10, 11))]
 
     def between():
         if spare:
-            for call in spare.pop(0):
-                call[0](*call[1:])
+            run(spare.pop(0))
 
     def first_step(c):
-        tn, nat, off, la = "tn%d" % c, "nat%d" % c, "off%d" % c, "la%d" % c
-        src = [V("dm", 0, 1, 96 * i, 96 * i + 32) for i in range(2)]
-        wide = [(ts, V("nbm", 32 * i, 32 * i + 32, 32 * q, 32 * q + 32), V("zero", 0, 32, 96 * i, 96 * i + 32), src[i], None, A.add)
-                for i in range(2) for q in range(2)]
+        m, u, off = "m%d" % c, "u%d" % c, "off%d" % c
+        low = rank >> (c - 1) & 1
         return [
-            [(cp, V(tn, 98, 99), V(la, 0, 1)),
-             (ts, V("colm", 1, 2, 32, 64), V(tn, 64, 65, 32, 64), -0.5, None, A.add),
-             (ts, V("colm", 1, 2, 0, 32), V(la, 0, 1, 0, 32), -0.5, None, A.add)],
-            [(tt, V("dgm", 0, 128), V("ps", 2560, 2688), V("negi", 0, 128), A.mult),
-             (ts, V("pnm", 0, 32), V("zero", 0, 32), V(tn, 98, 99), None, A.add)],
-            [(total, V("dm", 0, 1), V("dgm", 0, 128)), (tp, V(nat, 64, 96), V("pnm", 0, 32))],
-            wide[:3] + [(ac, V("taum", 1 + 32 * i, 33 + 32 * i, 0, 64), V(nat, early[i], early[i] + 32, 0, 64), F.Sign, None,
-                         V("colm", 1, 2, 0, 64)) for i in range(2)],
-            wide[3:] + [(cp, V("colm", 0, 1, 32 * i, 32 * i + 32), src[i]) for i in range(2)],
-            [(tp, V("nrm", 0, 64, 0, 64), V("nbm", 0, 64, 0, 64)),
-             (tt, V("sigm", 0, 65, 0, 64), V("taum", 0, 65, 0, 64), V("taum", 1, 66, 0, 64), A.mult)],
-            [(ac, V("junkm", 0, 64, 0, 64), V("nrm", 0, 64, 0, 64), F.Sign, None, V("colm", 0, 1, 0, 64), V("accm", 0, 1, 0, 64)),
-             (ts, V("eqm", 0, 64, 0, 64), V("nrm", 0, 64, 0, 64), V("colm", 0, 1, 0, 64), None, A.is_equal)],
-            [(scan, V("eom", 0, 65, 0, 64), V("sigm", 0, 65, 0, 64), V("eqm", 0, 65, 0, 64), A.mult, A.add)],
-            [(ts, V("ksm", 0, 32, 0, 64), V("kcm", 0, 32, 0, 64), V("accm", 0, 1, 0, 64), None, A.subtract)],
-            [(ts, V("prem", 0, 32, 0, 64), V("ksm", 0, 32, 0, 64), V("eom", 64, 65, 0, 64), V("pbm", 0, 1, 0, 64), A.is_equal, A.mult)],
-            [(tp, V("trm", 0, 32, 0, 64), V("prem", 0, 32, 0, 64))],
-            [(scan, V("tom", 0, 38, 0, 64), V("zero", 0, 38, 0, 64), V("trm", 0, 38, 0, 64), A.add, A.add)],
-            [(ts, V(off, 0, 5, 32 * q, 32 * q + 32), V("tom", 33, 38, 0, 32), V("tom", 31, 32, 32, 64), None, A.add) for q in range(2)],
-            [(ts, V(off, 0, 5, 32 * q, 32 * q + 32), V("tom", 33, 38, 0, 32), V("tom", 31, 32, 32, 64), None, A.add) for q in (2, 3)]]
+            [(tt, V("dgm", 0, 32, 96 * i, 96 * i + 32), bank(5, 96 * i, 96 * i + 32, 96 * i, 96 * i + 32),
+              V("negi", 96 * i, 96 * i + 32, 96 * i, 96 * i + 32), A.mult) for i in range(2)],
+            [(scan, V("nbm", 0, 64, 32 - 32 * i, 64 - 32 * i), V("zero", 0, 64, 96 * i, 96 * i + 32),
+              V("dgm", 0, 64, 96 * i, 96 * i + 32), A.add, A.add) for i in range(2)],
+            [(tp, V("nrm", 0, 32, 0, 64), V("nbm", 32, 64, 0, 64))],
+            [(ts, V("eqm", 0, 16, 32 * i, 32 * i + 32), V("nrm", 0, 16, 32 * i, 32 * i + 32),
+              V("nbm", 63, 64, 32 - 32 * i, 64 - 32 * i), None, A.is_le if i == low else A.is_lt) for i in range(2)],
+            [(scan, V("eom", 0, LM, 0, 64), V("sigm", 0, LM, 0, 64), V("eqm", 0, LM, 0, 64), A.mult, A.add, V("idm", 0, 1, 0, 64))],
+            [(tp, V("trm", 0, 32, 0, 64), V("eom", 16, 48, 0, 64))]
+            + [(ts, V("fl", 0, 1, 96 * i, 96 * i + 32), V("eom", 16, 17, 32 * i, 32 * i + 32), 8192.0, BIG, A.is_lt, A.mult)
+               for i in range(2)],
+            [(red, V("amm", 0, 1, 0, 64), V("trm", 0, 33, 0, 64), A.min, True)],
+            [(ts, V(off, 0, 3, 32 * q, 32 * q + 32), V("cbm", 0, 3, 0, 32), V("amm", 0, 1, 0, 32), V("amm", 0, 1, 32, 64), A.add, A.add)
+             for q in range(4)],
+            [(pick, u, 0, m, 96, 128, V(off, 0, 1))]]
+
+    def turn(z, i, k):
+        w = 64 if i == 0 or z == 0 else 32
+        po, pi = ((0, 128), (0, 64), (64, 128))[k], ((0, 128), (64, 128), (0, 64))[k]
+        d = 128 * i + (w if k else 0)
+        tp(V("nr", d, d + w, *po), V("nb", at(2 * i), at(2 * i) + w, *pi))
+
+    def gram(c, b0, b1):
+        n, starts, seq = shape[min(c, 1)][:3]
+        for b, st in enumerate(starts):
+            if b0 == 0:
+                mm(b, n, "m%d" % c, 32 * st, "m%d" % c, 32)
+        for b, st in list(enumerate(starts))[b0:b1]:
+            ac(V("ga", b * n, b * n + n), bank(b, 0, n), F.Abs)
+            q = 0
+            while q < 4:
+                e = q + 1
+                while e < 4 and seq[st + e] == seq[st + e - 1] + 1:
+                    e += 1
+                c0 = b * n + 32 * seq[st + q]
+                v = V("ga", c0, c0 + 32 * (e - q), 0, 32 * e)
+                op("g", lambda: g.affine_select(ap(v), ap(v), [[-1, 32 * (e - q)]], A.not_equal, BIG, -32 * q, 1), [v], [v])
+                q = e
 
     def choice(c):
         z = min(c, 1)
-        n, starts, seq, first, ranked = shape[z]
-        nw, t, tail = len(starts), str(z), (96, 64)[z]
-        H, m0 = 32 * nw, 32 * first
+        n, starts, seq, ranked, part = shape[z]
+        nw, t, L = len(starts), str(z), n + 33
         m, nx, off = "m%d" % c, "m%d" % (c + 1), "off%d" % c
         nat, natx, tnx = "nat%d" % c, "nat%d" % (c + 1), "tn%d" % (c + 1)
         last = c == 2
         place = (0, 32, 64) if last else (192, 160, 128)
         placen = place if last else (160, 128, 96)
-        pair = [V(off, 10 * i + 4, 10 * i + 6) for i in range(3)]
-        col = [V("nb", block(b)[3], block(b)[3] + 1) for b in ranked]
+        col = [V("nb", at(b), at(b) + 1) for b in ranked]
         peer, ar, ab = peers.get(c + 1), "ar%d" % (c + 1), "ab%d" % (c + 1)
-        held = (2, nw - 2)
+        low = c and rank >> (c - 1) & 1 == 0
 
-        def runs(b):
-            st, q, out = starts[b], 0, []
-            while q < 4:
-                e = q + 1
-                while e < 4 and seq[st + e] == seq[st + e - 1] + 1:
-                    e += 1
-                out.append((q, e, 32 * seq[st + q]))
-                q = e
-            return out
+        def lst(s, k=1, b=0):
+            c0 = (4 * s + b, 2 + 2 * s)[z]
+            return V(off, c0, c0 + k)
 
-        def diagonal(b):
-            for q, e, c0 in runs(b):
-                tt(V("dgo", 128 * b + 32 * q, 128 * b + 32 * e), V("ps", 512 * b + c0, 512 * b + c0 + 32 * (e - q)),
-                   V("negi", 32 * q, 32 * e), A.mult)
+        def winners(s, numbers=ac):
+            d = 16 * (s % 2)
+            pick(nx, place[s // 2] + d, m, 32, n, lst(s))
+            o = V(natx, placen[s // 2] + d, placen[s // 2] + d + 16)
+            if numbers is ac:
+                ac(o, V(nat, 0, n), F.Identity, off=lst(s))
+            else:
+                cp(o, V(nat, 0, n), off=lst(s))
 
-        def magnitudes(b):
-            ac(V("ga", b * n, b * n + n), V("ps", 512 * b, 512 * b + n), F.Abs)
-
-        def raise_diagonal(b):
-            for q, e, c0 in runs(b):
-                v = V("ga", b * n + c0, b * n + c0 + 32 * (e - q), 0, 32 * e)
-                op("g", lambda: g.affine_select(ap(v), ap(v), [[-1, 32 * (e - q)]], A.not_equal, BIG, -32 * q, 1), [v], [v])
-
-        def diagonal_sum(b):
-            total(V("dg", b, b + 1), V("dgo", 128 * b, 128 * b + 128))
-
-        def turn(i, k):
-            w = 32 * held[i]
-            po, pi = ((0, 128), (0, 64), (64, 128))[k], ((0, 128), (64, 128), (0, 64))[k]
-            d = 64 * i + (H if k else 0)
-            tp(V("nr", d, d + w, *po), V("nb", 96 * i + 16, 96 * i + 16 + w, *pi))
-
-        if c:
-            tn = "tn%d" % c
-            ts(V("lr", 0, 16), V("nat0", 0, n), -float(P * rank), None, A.add, off=V(off, 0, 1))
-            for b in range(nw):
-                ts(V("gt", 16 * b, 16 * b + 16), V("lr", 0, 16), V("pos1", b, b + 1), BIG, A.is_equal, A.mult)
-            scan(V("sc", 0, 16 * nw), V("keep", 0, 16 * nw), V("gt", 0, 16 * nw), A.mult, A.max)
-            for b in range(nw):
-                ts(block(b), V("zero", 0, 32), V("sc", 16 * b + 15, 16 * b + 16), None, A.add)
-        for b in range(nw):
-            mm(b, n, m, 32 * starts[b], m, m0)
-        if c == 0:
-            multipliers(0, 0)
-            for b in range(nw):
-                diagonal(b)
-            for b in range(nw):
-                magnitudes(b)
-                raise_diagonal(b)
-            for b in range(nw):
-                diagonal_sum(b)
-        else:
-            for b in range(nw):
-                magnitudes(b)
-            diagonal(0)
-            diagonal(1)
+        def products(s, call):
+            for o in range(O):
+                y, a = V("ysb", W * o + 16 * s, W * o + 16 * s + 16), V("yall", n * o, n * o + n)
+                if call is ac:
+                    ac(y, a, F.Identity, off=lst(s))
+                else:
+                    cp(y, a, off=lst(s))
 
         for s in range(z, S):
-            if s:
-                o0 = 10 * ((s - 1) // 2) + 6 * ((s - 1) % 2)
-                if s > z:
-                    for i in range(2):
-                        c0, k = 96 * i + 32, held[i]
-                        tt(V("gh", c0, c0 + 16 * k), V("ga", 0, nw * n), V("nb", c0, c0 + 16 * k), A.add,
-                           off=V(off, o0 + 2 * i, o0 + 2 * i + k))
-                else:
-                    cp(V("gt", 0, 16 * nw), V("ga", 0, nw * n), off=V(off, o0, o0 + nw))
-                if s in (2, 4):
-                    i = s // 2 - 1
-                    pick(nx, place[i], m, m0, n, pair[i])
-                    ac(V(natx, placen[i], placen[i] + 32), V(nat, 0, n), F.Identity, off=pair[i])
-                    if last and i == 0:
-                        repeat(nx, 96, 0, "da3")
-                        repeat(nx, 64, 0, "db3")
-                    elif last:
-                        mm(4, P, nx, 0, "m0")
-                        dma("y", T.oc[:, 0:256], V(nx + "q", 0, 64))
-                    elif i == 0:
-                        send(peer, [(V(nx + "q", 96, 128), V(nx + "q", 192, 224))], ab)
-                        send(peer, [(V(nx + "s", 96, 128), V(nx + "s", 192, 224))], ab)
-                        repeat(nx, 160, 192, "dc%d" % (c + 1))
-                        repeat(nx, 128, 192, "dd%d" % (c + 1))
-                        repeat(nx, 224, 192, "da%d" % (c + 1))
-                    else:
-                        repeat(nx, 0, 160, "db%d" % (c + 1))
-                        send(peer, [(V(nx + "q", 64, 96), V(nx + "q", 160, 192))], ar)
-                elif s == 5 and not last:
-                    pick(nx, 128, m, m0, n, V(off, 24, 25))
-                    send(peer, [(V(nx + "q", 32, 48), V(nx + "q", 128, 144))], ar)
-                elif s == 1 and c:
-                    for b in range(nw):
-                        raise_diagonal(b)
-                    diagonal(2)
-                    cp(V(tn, 96, 98), V("ln%d" % c, 0, 2))
-                else:
-                    between()
             if s > z:
+                if z == 0:
+                    for i in range(2):
+                        tt(V("gh", 96 * i + 32, 96 * i + 64), V("ga", 0, nw * n), V("nb", at(2 * i) + 16, at(2 * i) + 48), A.add,
+                           off=lst(s - 1, 2, 2 * i))
+                else:
+                    for b in range(nw):
+                        c0, d = 96 * (b // 2) + 32 + 16 * (b % 2), at(b) + 16 - 16 * (b % 2)
+                        tt(V("gh", c0, c0 + 16), V("ga", b * n, b * n + n), V("nb", d, d + 16), A.add, off=lst(s - 1))
                 for b in range(nw):
-                    c0, way = 96 * (b // 2) + 48 * (b % 2), 1 - 2 * (b % 2)
-                    scan(V("nb", c0, c0 + 48, step=way), V("zero", 0, 48), V("gh", c0, c0 + 48, step=-way), A.add, A.max, LOW)
-            elif z:
-                scan(V("sc", 0, 16 * nw), V("keep", 0, 16 * nw), V("gt", 0, 16 * nw), A.mult, A.max)
-                for b in range(nw):
-                    diagonal_sum(b)
-                for b in range(2):
-                    ts(V("pn", 32 * b, 32 * b + 32), V("zero", 0, 32), V(tn, 96 + b, 97 + b), None, A.add)
-                ts(V("ncol", 0, 32), V(tn, 0, 99), -0.5, None, A.add, off=V("colo", 0, 2))
-                tp(V(nat, 0, 64), V("pn", 0, 64))
-                signs(c)
-                for b in range(nw):
-                    ts(block(b), block(b), V("dg", b, b + 1), V("sc", 16 * b + 15, 16 * b + 16), A.add, A.add)
-            else:
-                for b in range(nw):
-                    ts(block(b), V("zero", 0, 32), V("dg", b, b + 1), None, A.add)
-            if s == 0:
-                multipliers(0, 1)
-            else:
-                between()
-            for i, k in (((0, 0), (0, 1), (1, 0), (0, 2), (1, 1), (1, 2)), ((0, 0), (1, 0), (0, 1), (0, 2), (1, 1), (1, 2)))[z]:
-                turn(i, k)
-            for part in range(2):
-                for a in range(2):
-                    ac(V("junk", 256 * a + part * H, 256 * a + part * H + H), V("nr", part * H, part * H + H), F.Sign,
-                       bias=col[a], accum=V("acc", 2 * a + part, 2 * a + part + 1))
-            for part in range(2):
-                for a in range(2):
-                    e0 = a * (n + 2) + part * H
-                    ts(V("eq" + t, e0, e0 + H), V("nr", part * H, part * H + H), col[a], None, A.is_equal)
-            if s == 1 and c:
+                    c0 = 96 * (b // 2) + 48 * (b % 2)
+                    scan(into(b, 16), V("zero", 0, 48), V("gh", c0, c0 + 48, step=2 * (b % 2) - 1), A.add, A.max, LOW)
+                winners(s - 1)
+                if last and s == 2:
+                    repeat(nx, 96, 0, "da3")
+                    repeat(nx, 64, 0, "db3")
+                elif last and s == 4:
+                    mm(6, P, nx, 0, "m0", 32)
+                    dma("y", T.oc[:, 0:256], V(nx + "q", 0, 64))
+                elif s == 2:
+                    send(peer, [(V(nx + "q", 96, 128), V(nx + "q", 192, 224))], ab)
+                    send(peer, [(V(nx + "s", 96, 128), V(nx + "s", 192, 224))], ab)
+                    repeat(nx, 160, 192, "dc%d" % (c + 1))
+                    repeat(nx, 128, 192, "dd%d" % (c + 1))
+                    repeat(nx, 224, 192, "da%d" % (c + 1))
+                    repeat("u%d" % (c + 1), 16, 32, "du%d" % (c + 1), "m0", 112)
+                elif s == 4:
+                    repeat(nx, 0, 160, "db%d" % (c + 1))
+                    send(peer, [(V(nx + "q", 64, 96), V(nx + "q", 160, 192))], ar)
+                elif s == 5 and not last:
+                    send(peer, [(V(nx + "q", 32, 48), V(nx + "q", 128, 144))], ar)
+            for i in range(2):
+                for k in range(3):
+                    turn(z, i, k)
+            for a in range(2):
+                lo, hi = part[a]
+                ac(V("junk", 256 * a, 256 * a + hi - lo), V("nr", lo, hi), F.Sign, bias=col[a], accum=V("acc", a, a + 1))
+            if s == z:
+                gram(c, nw - 1, nw)
+            (l0, h0), (l1, h1) = part
+            ts(V("eq" + t, l0, h0), V("nr", l0, h0), col[0], None, A.is_equal)
+            ts(V("eq" + t, L, L + l1), V("nr", 0, l1), col[1], None, A.is_lt if low else A.is_le)
+            if s == z and c:
                 multipliers(c, 0)
-                multipliers(c, 1)
-            elif s:
-                between()
+            ts(V("eq" + t, h0, n), V("nr", h0, n), col[0], None, A.is_le if low else A.is_lt)
+            ts(V("eq" + t, L + l1, L + n), V("nr", l1, n), col[1], None, A.is_equal)
             for a in range(2):
-                e0 = a * (n + 2)
-                scan(V("eo", e0, e0 + n + 1), V("sig", e0, e0 + n + 1), V("eq" + t, e0, e0 + n + 1), A.mult, A.add)
-                ts(V("ks", 32 * a, 32 * a + 32), V("kc" + t, 0, 32), V("acc", 2 * a, 2 * a + 1), V("acc", 2 * a + 1, 2 * a + 2),
-                   A.subtract, A.subtract)
-            if s == 4 and last:
-                ac(V("zsb", 0, P, 0, 64), V("ps", 2048, 2048 + P, 0, 64), F.Copy)
+                scan(V("eo", a * L, a * L + L, step=1 - 2 * a), V("sig" + t, a * L, a * L + L), V("eq" + t, a * L, a * L + L),
+                     A.mult, A.add, V("acc", a, a + 1))
+            if s == 0:
+                run(soon)
+                for f in fills:
+                    iota(f[1], [[0, f[1][4] - f[1][3]]], int(f[2]), 0)
+            elif c == 2 and s == 1:
+                winners(0)
+                for o in range(O):
+                    mm(3 + o, n, "w", 128 * o, m, 32)
+            elif c == 1 and s == 1:
+                winners(0)
+            elif c == 1 and s == 2:
+                quant("w", "wt", 0, 128)
+            elif s == 4 and not last:
+                tp(V(tnx, 0, 64), V(natx, 128, 192))
+            else:
+                between()
+            if last and s == 2:
+                for o in range(O):
+                    ac(V("yall", n * o, n * o + n), bank(3 + o, 0, n), F.Identity)
+            if last and s == 4:
+                ac(V("zsb", 0, P, 0, 64), bank(6, 0, P, 0, 64), F.Copy)
                 dma("y", T.z[0:64, :], V("zsb", 0, P, 0, 64))
-            for a in range(2):
-                e1 = a * (n + 2) + n
-                for p0, p1, d0, c0 in ((0, 96, 0, 32 * a), (96, 128, 32 * a, 64))[:2 - z]:
-                    ts(V("pre", c0, c0 + 32, d0, d0 + p1 - p0), V("ks", 32 * a, 32 * a + 32, p0, p1),
-                       V("eo", e1, e1 + 1, p0, p1), V("pb" + t, ranked[a], ranked[a] + 1, p0, p1), A.is_equal, A.mult)
-            if s == 2 and not last:
-                tp(V(tnx, 64, 96), V(natx, 160, 192))
+            if last and s >= 3:
+                for k in ((0, 1), (2, 3), (4,))[s - 3]:
+                    products(k, ac)
+                if s == 5:
+                    for o in range(O):
+                        dma("y", T.y[:, W * o:W * o + 80], V("ysb", W * o, W * o + 80))
+            if z == 0:
+                for h in range(2):
+                    tp(V("tr0", 64 * h, 64 * h + 64, 0, 64), V("eo", L - 32, L + 32, 64 * h, 64 * h + 64))
             else:
-                between()
-            tp(V("tr" + t, 0, tail, 0, 96), V("pre", 0, tail, 0, 96))
-            if s == 2 and not last:
-                cp(V("sa%d" % (c + 1), 0, 2), V(tnx, 64, 66))
-                send(peer, [(V("la%d" % (c + 1), 0, 2), V("sa%d" % (c + 1), 0, 2))], "ae%d" % (c + 1))
-            else:
-                between()
-            scan(V("to", 0, tail + 6, 0, 96), V("zero", 0, tail + 6, 0, 96), V("tr" + t, 0, tail + 6, 0, 96), A.add, A.add)
-            between()
+                tp(V("tr1", 0, 64, 0, 96), V("eo", L - 32, L + 32, 0, 96))
             if s == 3 and not last:
                 mm(5, 128, nx, 96, nx, 96)
+                assert not spare
                 spare.extend(first_step(c + 1))
-            o0, b0 = 10 * (s // 2) + 5 * (s % 2), tail + 1 - s % 2
+            if s == 4 and not last:
+                cp(V("sa%d" % (c + 1), 0, 2), V(tnx, 0, 64, step=32))
+                send(peer, [(V("la%d" % (c + 1), 0, 2), V("sa%d" % (c + 1), 0, 2))], "ae%d" % (c + 1))
+            if c == 1 and s == 2:
+                quant("w", "wt", 128, 256)
+            else:
+                between()
+            if z == 0:
+                red(V("am", 0, 1, 0, 64), V("tr0", 0, 129, 0, 64), A.min, True)
+            else:
+                red(V("am", 0, 1, 0, 96), V("tr1", 0, 64, 0, 96), A.min, True)
+            if c == 1 and s == 2:
+                quant("w", "wt", 256, 384)
+            else:
+                between()
             for q in range(4):
-                ts(V(off, o0, o0 + 5, 32 * q, 32 * q + 32), V("to", b0, b0 + 5, 0, 32),
-                   V("to", tail - 1, tail, 32, 64), V("to", tail - 1, tail, 64, 96), A.add, A.add)
+                o = lst(s, nw) if z == 0 else lst(s)
+                o = V(off, o[3], o[4], 32 * q, 32 * q + 32)
+                if z == 0:
+                    ts(o, V("cb0", 0, 4, 0, 32), V("am", 0, 1, 0, 32), V("am", 0, 1, 32, 64), A.add, A.add)
+                else:
+                    ts(o, V("am", 0, 1, 0, 32), V("am", 0, 1, 32, 64), V("am", 0, 1, 64, 96), A.min, A.min)
+            if s < 5:
+                between()
 
         if last:
-            pick(nx, 64, m, m0, n, pair[2])
-            cp(V(natx, 64, 96), V(nat, 0, n), off=pair[2])
+            pick(nx, 80, m, 32, n, lst(5))
+            products(5, cp)
+            ac(V(natx, 80, 96), V(nat, 0, n), F.Identity, off=lst(5))
             return
-        pick(nx, 144, m, m0, n, V(off, 26, 27))
+        c += 1
+        u, la, ln = "u%d" % c, "la%d" % c, "ln%d" % c
+        winners(5, cp)
         send(peer, [(V(nx + "q", 48, 64), V(nx + "q", 144, 160)), (V(nx + "s", 32, 96), V(nx + "s", 128, 192))], ar)
-        cp(V(natx, 96, 128), V(nat, 0, n), off=pair[2])
-        between()
-        tp(V(tnx, 0, 64), V(natx, 96, 160))
-        between()
-        cp(V("sn%d" % (c + 1), 0, 2), V(tnx, 0, 64, step=32))
-        send(peer, [(V("ln%d" % (c + 1), 0, 2), V("sn%d" % (c + 1), 0, 2))], "an%d" % (c + 1))
         while spare:
             between()
-        if c == 1:
-            quant("w", "wt", 0, 128 * O)
+        cp(V("lf", 0, 2), V(la, 0, 2))
+        tp(V(tnx, 64, 96), V(natx, 96, 128))
+        send(peer, [(V(ln, 0, 1), V(tnx, 64, 65))], "an%d" % c)
+        mm(6, 128, nx, 96, nx, 96)
+        mm(7, 128, nx, 96, u, 0)
+        for i in range(2):
+            ts(V("pn", 32 + 32 * i, 64 + 32 * i), V("zero", 0, 32), V("lf", i, i + 1), None, A.add)
+        ts(V("ncol", 1, 2, 32, 64), V(tnx, 0, 1, 32, 64), -0.5, None, A.add)
+        ts(V("ncol", 1, 2, 64, 128), V(tnx, 32, 33, 64, 128), -0.5, None, A.add)
+        ts(V("ncol", 1, 2, 0, 32), V(tnx, 64, 65, 0, 32), -0.5, None, A.add)
+        tp(V(natx, 32, 96), V("pn", 32, 96))
+        tt(V("dgy", 0, 128), bank(6, 0, 128), V("negi", 0, 128), A.mult)
+        signs(c, 1)
+        red(V("dy", 0, 1), bank(7, 0, 16), A.max, True)
+        ts(V("ncol", 0, 1, 32, 64), V("lf", 0, 1, 32, 64), -0.5, None, A.add)
+        ts(V("ncol", 0, 1, 64, 96), V("lf", 1, 2, 64, 96), -0.5, None, A.add)
+        red(V("dy", 1, 2), V("dgy", 0, 128), A.add)
+        multipliers(c, 1)
+        ts(V("dy", 2, 3), V("dy", 1, 2), V("fl", 0, 1), None, A.add)
+        for b, p0, p1, s0 in ((0, 64, 128, 0), (1, 0, 32, 64), (1, 96, 128, 0), (2, 0, 32, 32), (2, 32, 64, 64), (2, 64, 96, 96),
+                              (2, 96, 128, 96)):
+            s1 = s0 + p1 - p0
+            ts(block(b, p0, p1), V("zero", 0, 32, p0, p1), V("dy", 0, 1, s0, s1), V("dy", 2, 3, s0, s1), A.add, A.add)
+        mm(3, 128, nx, 32, nx, 32)
+        mm(4, 128, nx, 32, u, 0)
+        for q in range(2):
+            tt(V("dga", 0, 32, 32 * q, 32 * q + 32), bank(3, 32 * q, 32 * q + 32, 32 * q, 32 * q + 32),
+               V("negi", 32 * q, 32 * q + 32, 32 * q, 32 * q + 32), A.mult)
+        red(V("dy", 3, 4, 0, 64), bank(4, 0, 16, 0, 64), A.max, True)
+        ts(V("pn", 0, 32), V("zero", 0, 32), V(ln, 0, 1), None, A.add)
+        ts(V("ncol", 0, 1, 0, 32), V(ln, 0, 1, 0, 32), -0.5, None, A.add)
+        for b, p0, p1, s0 in ((0, 0, 64, 0), (1, 32, 64, 0), (1, 64, 96, 32)):
+            s1 = s0 + p1 - p0
+            scan(into(b, 32, p0, p1), V("zero", 0, 64, s0, s1), V("dga", 0, 64, s0, s1), A.add, A.add, V("dy", 3, 4, s0, s1))
+        gram(c, 0, 2)
+        tp(V(natx, 0, 32), V("pn", 0, 32))
+        signs(c, 0)
+
+    for h in range(2):
+        quant("m0", "xt", 160 * h, 160 * h + 160)
+        for b in (2 * h, 2 * h + 1):
+            mm(4 + b, 128, "m0", 32 * shape[0][1][b], "m0", 32 * shape[0][1][b])
+    gram(0, 0, 3)
+    run(late)
+    for h in range(2):
+        for b in (2 * h, 2 * h + 1):
+            c0 = 320 * h + 192 * (b % 2)
+            tt(V("dgo", c0, c0 + 128), bank(4 + b, 0, 128), V("negi", 0, 128), A.mult)
+        multipliers(0, h)
+        for b in (2 * h, 2 * h + 1):
+            c0 = 320 * h + 160 * (b % 2)
+            scan(into(b, 128), V("zero", 0, 160), V("dgo", c0, c0 + 160, step=1 - 2 * (b % 2)), A.add, A.add)
 
     for c in range(3):
         choice(c)
@@ -546,20 +603,19 @@ def rank_program(g, core, T, topo):
     def scales_out(q, k):
         dma(q, T.osc[4 * k:4 * k + 4, :], V("m3s", 0, W, 32 * k, 32 * k + 4))
 
-    for o in range(O):
-        mm(5 + o, 128, "w", 128 * o, "m3")
-    mm(4, P, "m3", 0, "m0")
+    for h in range(2):
+        mm(6 + h, 128, "m3", 0, "m0", 32 + 128 * h)
     dma("y", T.oc[:, 256:4 * W], V("m3q", 64, W))
-    scales_out("y", 0)
-    dma("s", T.wn[:], V("nat3", 0, W, 0, 1))
+    scales_out("s", 0)
+    scales_out("s", 1)
     for o in range(O):
-        cp(V("ysb", W * o, W * o + W), V("ps", 512 * (5 + o), 512 * (5 + o) + W))
-    ac(V("zsb", 0, P, 64, W), V("ps", 2048, 2048 + P, 64, W), F.Copy)
-    dma("y", T.y[:], V("ysb", 0, O * W))
+        dma("y", T.y[:, W * o + 80:W * o + W], V("ysb", W * o + 80, W * o + W))
+    dma("s", T.wn[:], V("nat3", 0, W, 0, 1))
+    ac(V("zsb", 128, P, 64, W), bank(7, 0, 128, 64, W), F.Copy)
+    cp(V("zsb", 0, 128, 64, W), bank(6, 0, 128, 64, W))
+    scales_out("y", 2)
+    scales_out("y", 3)
     dma("s", T.z[64:W, :], V("zsb", 0, P, 64, W))
-    scales_out("y", 1)
-    scales_out("s", 2)
-    scales_out("s", 3)
     g.sync.wait_ge(T.sem.st, count["st"])
     g.wait_ge(T.sem.sent, sent[0])
     for k in own_sem:

from concourse.bass import DstId, RemoteDMATransfer
from concourse.mybir import dt, AluOpType as A, AxisListType, ActivationFunctionType as F

P, K, S, O = 256, 16, 6, 3
W = K * S
BIG = 1e29
LOW = -9e29
Q4, U8, F32, BF, U16, I32 = "float8_e4m3fn_x4", "uint8", "float32", "bfloat16", "uint16", "int32"
L0, L1, LM = 256 + 33, 192 + 33, 16 + 32


def _sb(n, d):
    return ("sbuf", [128, n], d)


SCRATCH = {
    "xt": _sb(4 * (P + 64), BF), "m0q": _sb(P + 64, Q4), "m0s": _sb(P + 64, U8),
    "wt": _sb(512 * O, BF), "wq": _sb(128 * O, Q4), "ws": _sb(128 * O, U8),
    "m1q": _sb(256, Q4), "m1s": _sb(256, U8), "m2q": _sb(256, Q4), "m2s": _sb(256, U8),
    "m3q": _sb(128, Q4), "m3s": _sb(128, U8),
    "u1q": _sb(128, Q4), "u1s": _sb(128, U8), "u2q": _sb(128, Q4), "u2s": _sb(128, U8),
    "ps": ("psum", [128, 4096], F32),
    "ga": _sb(1024, F32), "nb": _sb(640, F32), "gh": _sb(192, F32), "nr": _sb(256, F32),
    "dgo": _sb(640, F32), "dgy": _sb(128, F32), "dga": _sb(64, F32), "dy": _sb(4, F32), "negi": _sb(128, F32),
    "zero": _sb(160, F32), "fl": _sb(1, F32),
    "eq0": _sb(2 * L0, BF), "eq1": _sb(2 * L1, BF), "sig0": _sb(2 * L0, BF), "sig1": _sb(2 * L1, BF),
    "tau0": _sb(264, BF), "tau1": _sb(296, BF), "eo": _sb(2 * L0, BF), "junk": _sb(512, BF),
    "tr0": _sb(130, BF), "tr1": _sb(64, BF), "am": _sb(1, F32), "acc": _sb(2, F32), "cb0": _sb(4, F32),
    "dgm": _sb(64, F32), "nbm": _sb(64, F32), "nrm": _sb(32, F32), "eqm": _sb(LM, BF), "sigm": _sb(LM, BF),
    "eom": _sb(LM, BF), "trm": _sb(34, BF), "amm": _sb(1, F32), "idm": _sb(1, F32), "cbm": _sb(3, F32),
    "ii": _sb(2, I32), "pf": _sb(2, F32), "pr": _sb(1, F32),
    "pos0": _sb(4, F32), "pos1": _sb(4, F32), "blk0": _sb(8, F32), "blk1": _sb(8, F32),
    "perm0": _sb(16, U16), "perm1": _sb(16, U16),
    "off0": _sb(24, U16), "off1": _sb(14, U16), "off2": _sb(14, U16),
    "nat0": _sb(256, F32), "nat1": _sb(192, F32), "nat2": _sb(192, F32), "nat3": _sb(96, F32),
    "tn1": _sb(96, F32), "tn2": _sb(96, F32), "pn": _sb(96, F32), "ncol": _sb(2, F32), "lf": _sb(2, F32),
    "ln1": _sb(1, F32), "ln2": _sb(1, F32), "sa1": _sb(2, U16), "sa2": _sb(2, U16), "la1": _sb(2, U16), "la2": _sb(2, U16),
    "yall": _sb(O * 192, F32), "ysb": _sb(O * W, F32), "zsb": _sb(P, F32),
}
SEMAPHORES = ["cv", "cs", "ct", "cg", "lxa", "lxb", "lw", "ar1", "ar2", "ab1", "ab2", "an1", "an2", "ae1", "ae2", "sent",
              "da1", "db1", "dc1", "dd1", "da2", "db2", "dc2", "dd2", "da3", "db3", "du1", "du2", "st"]


def V(name, c0, c1, p0=0, p1=128, step=1):
    return (name, p0, p1, c0, c1, step)


def at(b):
    return 320 * (b // 2) + 128 + 32 * (b % 2)


def block(b, p0=0, p1=128):
    return V("nb", at(b), at(b) + 32, p0, p1)


def into(b, lead, p0=0, p1=128):
    if b % 2 == 0:
        return V("nb", at(b) - lead, at(b) + 32, p0, p1)
    return V("nb", at(b), at(b) + 32 + lead, p0, p1, -1)


def rank_program(g, core, T, topo):
    rank = T.rank_of(core)
    if rank is None:
        return
    queue = {"v": g.vector, "s": g.scalar, "t": g.tensor, "g": g, "y": g.sync}
    own_sem = {"v": "cv", "s": "cs", "t": "ct", "g": "cg"}
    count = {}
    known = {k: {} for k in queue}
    seen = {}

    def ap(v):
        if v[5] == -1:
            return T[v[0]][v[1]:v[2], v[4] - 1:(v[3] - 1 if v[3] else None):-1]
        return T[v[0]][v[1]:v[2], v[3]:v[4]:v[5]] if v[5] != 1 else T[v[0]][v[1]:v[2], v[3]:v[4]]

    def box(v):
        if v[0] == "ps":
            return (0, 128, v[3] // 512 * 512, (v[4] + 511) // 512 * 512)
        return (v[1], v[2], v[3], v[4])

    def wait(q, h):
        sem, val, clock = h
        if known[q].get(sem, 0) < val:
            queue[q].wait_ge(T.sem[sem], val)
            known[q][sem] = val
            for k in clock:
                if known[q].get(k, 0) < clock[k]:
                    known[q][k] = clock[k]

    def note(v, writes, q, h):
        b = box(v)
        old = seen.get(v[0], [])
        if writes and v[5] in (1, -1):
            old = [e for e in old if not (b[0] <= e[0] and e[1] <= b[1] and b[2] <= e[2] and e[3] <= b[3])]
        seen[v[0]] = old + [b + (writes, q, h)]

    def order(q, reads, writes):
        need = {}
        for vs, wr in ((reads, False), (writes, True)):
            for v in vs:
                b = box(v)
                for e in seen.get(v[0], []):
                    if b[0] < e[1] and e[0] < b[1] and b[2] < e[3] and e[2] < b[3]:
                        if wr or e[4] or (v[0] == "ps" and e[5] != q):
                            h = e[6]
                            if h[0] not in need or need[h[0]][1] < h[1]:
                                need[h[0]] = h
        for k in sorted(need, key=lambda k: k == own_sem.get(q)):
            wait(q, need[k])

    def op(q, call, reads, writes, sem=None, inc=1):
        order(q, reads, writes)
        sem = sem or own_sem[q]
        call().then_inc(T.sem[sem], inc)
        count[sem] = count.get(sem, 0) + inc
        h = (sem, count[sem], dict(known[q]))
        for v in reads:
            note(v, False, q, h)
        for v in writes:
            note(v, True, q, h)
        return h

    vec, act = g.vector, g.scalar

    def isv(a):
        return isinstance(a, tuple)

    def ts(out, in0, s1, s2, op0, op1=None):
        rd = [a for a in (in0, s1, s2) if isv(a)]
        a1, a2 = (ap(s1) if isv(s1) else s1), (ap(s2) if isv(s2) else s2)
        if op1 is None:
            return op("v", lambda: vec.tensor_scalar(ap(out), ap(in0), a1, None, op0), rd, [out])
        return op("v", lambda: vec.tensor_scalar(ap(out), ap(in0), a1, a2, op0, op1), rd, [out])

    def tt(out, in0, in1, o, off=None):
        a0 = ap(in0) if off is None else ap(in0).indirect(ap(off))
        return op("v", lambda: vec.tensor_tensor(ap(out), a0, ap(in1), o), [a for a in (in0, in1, off) if a], [out])

    def cp(out, in0, off=None):
        a0 = ap(in0) if off is None else ap(in0).indirect(ap(off))
        return op("v", lambda: vec.tensor_copy(ap(out), a0), [a for a in (in0, off) if a], [out])

    def ms(out, c):
        return op("v", lambda: vec.memset(ap(out), c), [], [out])

    def tp(out, in0):
        return op("v", lambda: vec.transpose(ap(out), ap(in0)), [in0], [out])

    def scan(out, d0, d1, o0, o1, init=0.0):
        a = ap(init) if isv(init) else init
        return op("v", lambda: vec.tensor_tensor_scan(ap(out), ap(d0), ap(d1), a, o0, o1),
                  [d0, d1] + [init] * isv(init), [out])

    def red(out, in0, o, size=False):
        return op("v", lambda: vec.tensor_reduce(ap(out), ap(in0), AxisListType.X, o, apply_absolute_value=size), [in0], [out])

    def quant(m, src, c0, c1):
        o, s, i = V(m + "q", c0, c1), V(m + "s", c0, c1), V(src, 4 * c0, 4 * c1)
        return op("v", lambda: vec.quantize_mx(ap(o), ap(s), ap(i)), [i], [o, s])

    def ac(out, in0, func, off=None, bias=None, accum=None):
        a0 = ap(in0) if off is None else ap(in0).indirect(ap(off))
        kw = {}
        if bias is not None:
            kw["bias"], kw["scale"] = ap(bias), -1.0
        if accum is not None:
            kw["accum_out"] = ap(accum)
        return op("s", lambda: act.activation(ap(out), a0, func, **kw), [a for a in (in0, off, bias) if a],
                  [a for a in (out, accum) if a])

    def iota(out, pattern, base, cm):
        if SCRATCH[out[0]][2] == I32:
            return op("g", lambda: g.iota(ap(out), pattern, base, cm), [], [out])
        return op("g", lambda: g.iota(ap(out), pattern, base, cm, allow_small_or_imprecise_dtypes=True), [], [out])

    def mm(bank, n, lq, l0, rq, r0=0):
        a, b = (V(lq + "q", l0, l0 + 128), V(lq + "s", l0, l0 + 128)), (V(rq + "q", r0, r0 + n), V(rq + "s", r0, r0 + n))
        out = V("ps", 512 * bank, 512 * bank + n)
        return op("t", lambda: g.tensor.matmul_mx(ap(out), ap(a[0]), ap(a[1]), ap(b[0]), ap(b[1]), True, True),
                  list(a + b), [out])

    def bank(b, c0, c1, p0=0, p1=128):
        return V("ps", 512 * b + c0, 512 * b + c1, p0, p1)

    def pick(dst, d0, src, s0, n, off):
        o, i = V(dst + "q", d0, d0 + 16), V(src + "q", s0, s0 + n)
        op("v", lambda: vec.tensor_copy(ap(o).bitcast(dt.uint32), ap(i).bitcast(dt.uint32).indirect(ap(off))), [i, off], [o])
        ac(V(dst + "s", d0, d0 + 16), V(src + "s", s0, s0 + n), F.Copy, off=off)

    def raw(v):
        return ap(v).bitcast(dt.uint8) if SCRATCH[v[0]][2] == Q4 else ap(v)

    def dma(q, out, v):
        return op(q, lambda: queue[q].dma_start(out, raw(v)), [v], [], sem="st", inc=16)

    def repeat(m, d0, s0, sem, src=None, k=32):
        hs = []
        for e in "qs":
            o, i = V(m + e, d0, d0 + k), V((src or m) + e, s0, s0 + k)
            order("y", [i], [o])
            g.sync.dma_start(raw(o), raw(i)).then_inc(T.sem[sem], 16)
            hs.append((o, i))
        h = (sem, 32, dict(known["y"]))
        for o, i in hs:
            note(i, False, "y", h)
            note(o, True, "y", h)

    sent = [0]

    def bits(es):
        return sum(1 << e for e in es)

    def send(peer, pieces, sem):
        order("g", [s for d, s in pieces], [])
        rid, pid = topo.addr(peer)[:2]
        es = topo.engines(core, peer)
        if len(pieces) == 1:
            g.remote_dma(raw(pieces[0][0]), raw(pieces[0][1]), T.sem[sem], T.sem.sent, pid, rid, bits(es))
        else:
            k = len(es) // len(pieces)
            g.remote_dma_fused([RemoteDMATransfer(dst_ids=[DstId(rid=rid, pnc=pid)], dma_engine_mask=bits(es[k * i:k * i + k]),
                                                  remote_sem=T.sem[sem], src=raw(s), dst=raw(d))
                                for i, (d, s) in enumerate(pieces)], local_sem=T.sem.sent)
        sent[0] += len(es)

    def run(calls):
        for call in calls:
            call[0](*call[1:])

    peers = {c: T.cores[rank ^ (1 << (c - 1))] for c in (1, 2)}
    for c in (1, 2):
        ne = len(topo.engines(peers[c], core))
        for e in "qs":
            note(V("m%d%s" % (c, e), 32, 96), True, None, ("ar%d" % c, 3 * ne, {}))
            note(V("m%d%s" % (c, e), 96, 128), True, None, ("ab%d" % c, 2 * ne, {}))
        note(V("la%d" % c, 0, 2), True, None, ("ae%d" % c, ne, {}))
        note(V("ln%d" % c, 0, 1), True, None, ("an%d" % c, ne, {}))

    shape = {0: (256, (0, 1, 5, 6), (3, 0, 1, 2, 3, 4, 5, 6, 7, 4), (1, 2), ((0, 128), (128, 256))),
             1: (192, (1, 0, 4), (4, 0, 1, 2, 3, 4, 5, 5), (0, 2), ((0, 128), (32, 192)))}

    for sem, h in (("lxa", 0), ("lxb", 1)):
        g.sync.dma_start(ap(V("xt", 128 + 512 * h, 640 + 512 * h)), T.x[:, 512 * h:512 * h + 512]).then_inc(T.sem[sem], 16)
        g.scalar.dma_start(ap(V("xt", 1152 * h, 1152 * h + 128)), T.x[:, 384 + 128 * h:512 + 128 * h]).then_inc(T.sem[sem], 16)
        note(V("xt", 640 * h, 640 * h + 640), True, "y", (sem, 32, {}))
    wait("y", ("lxb", 32, {}))
    op("y", lambda: g.sync.dma_start(T.wt[:], T.w[:]), [], [V("wt", 0, 512 * O)], sem="lw", inc=16)

    iota(V("ii", 0, 2), [[0, 2]], 0, 1)
    iota(V("pos0", 0, 4), [[128, 2], [32, 2]], 0, 1)
    iota(V("nat0", 0, 256), [[1, 256]], P * rank, 0)
    iota(V("pr", 0, 1), [[0, 1]], P * rank, 1)
    iota(V("cb0", 0, 4), [[256, 4]], -256, 0)
    iota(V("pos1", 0, 4), [[96, 2], [-32, 2]], 0, 1)
    iota(V("cbm", 0, 3), [[32, 3]], -320, 0)

    def tail(e, c0, down):
        d = 512.0 if down else -512.0
        return [(ms, V(e, c0 + 1, c0 + 32), d), (ms, V(e, c0 + 16, c0 + 17), -15 * d)]

    def tables(z):
        n, starts, seq, ranked, part = shape[z]
        nw, t, L = len(starts), str(z), n + 33
        k1 = nw - 2
        m = [hi - lo for lo, hi in part]
        calls = []
        for b, st in enumerate(starts):
            for q in range(4):
                if seq[st + q] != st + q - 1:
                    v = V("pos" + t, b, b + 1, 32 * q, 32 * q + 32)
                    calls.append((ts, v, v, float(32 * (seq[st + q] - st - q + 1)), None, A.add))
        calls += [(ms, V("sig" + t, 0, 2 * L), 1.0),
                  (ms, V("tau" + t, 0, 1), 1.0), (ms, V("tau" + t, m[0] + 1, m[0] + 2), 0.5),
                  (ms, V("tau" + t, m[0] + 2, m[0] + 3), 2.0), (ms, V("tau" + t, m[0] + m[1] + 3, m[0] + m[1] + 4), 1.0),
                  (ts, V("blk" + t, 0, 2), V("pos" + t, 0, 2), V("pf", 0, 1), V("pf", 1, 2), A.subtract, A.add),
                  (ts, V("blk" + t, 4, 4 + k1), V("pos" + t, 2, 2 + k1), V("pf", 0, 1), V("pf", 1, 2), A.subtract, A.add),
                  (ms, V("sig" + t, n + 1, n + 2), 512.0), (ms, V("sig" + t, L, L + 1), 0.5),
                  (ms, V("sig" + t, L + n + 1, L + n + 2), 256.0)]
        for c0, k in ((0, 2), (4, k1)):
            calls += [(cp, V("blk" + t, c0 + k, c0 + 2 * k, 0, 64), V("blk" + t, c0, c0 + k, 64, 128)),
                      (cp, V("blk" + t, c0 + k, c0 + 2 * k, 64, 128), V("blk" + t, c0, c0 + k, 0, 64))]
        calls += [(ms, V("eq" + t, n, n + 1), m[0] / 2.0), (ms, V("eq" + t, L + n, L + n + 1), m[1] - 30.0)]
        calls += [(cp, V("perm" + t, 0, 4 * nw, step=2), V("blk" + t, 0, 2 * nw)),
                  (ts, V("perm" + t, 1, 4 * nw, step=2), V("blk" + t, 0, 2 * nw), 16.0, None, A.add)]
        for a in range(2):
            calls += tail("eq" + t, a * L + n + 1, a)
            calls.append((cp, V("eq" + t, a * L + n + 1, a * L + n + 2), V("pos" + t, ranked[a], ranked[a] + 1)))
        return calls

    def signs(c, a):
        z = min(c, 1)
        n, part = shape[z][0], shape[z][4]
        lo, hi = part[a]
        e0 = 1 + a * (part[0][1] + 2)
        ac(V("tau%d" % z, e0, e0 + hi - lo), V("nat%d" % c, 0, n), F.Sign,
           off=V("perm%d" % z, lo // 16, hi // 16), bias=V("ncol", a, a + 1))

    def multipliers(c, a):
        z = min(c, 1)
        n, part = shape[z][0], shape[z][4]
        lo, hi = part[a]
        e0, s0, k = a * (part[0][1] + 2), a * (n + 33) + lo, hi - lo + 1
        tt(V("sig%d" % z, s0, s0 + k), V("tau%d" % z, e0, e0 + k), V("tau%d" % z, e0 + 1, e0 + k + 1), A.mult)

    calls = tables(0)
    late = [f for f in calls if f[1][0] == "eq0"]
    late = late[2::3] + late[:2] + late[4::3] + late[3::3]
    free = [f for f in calls if f[0] is ms and f not in late]
    free += [(ms, V("dgo", 128, 192), 0.0), (ms, V("dgo", 448, 512), 0.0), (ms, V("tr0", 128, 129), 256.0)]
    chain = [f for f in calls if f[0] is not ms and f not in late]
    ms(V("zero", 0, 160), 0.0)
    run(free[:1])
    ts(V("ii", 0, 1), V("ii", 0, 1), 31, None, A.bitwise_and)
    ts(V("ii", 1, 2), V("ii", 1, 2), 15, None, A.bitwise_and)
    ts(V("pos0", 0, 2), V("pos0", 0, 2), -32.0, None, A.add)
    run(chain[1:2] + free[1:2])
    cp(V("pf", 0, 2), V("ii", 0, 2))
    run(chain[:1] + free[2:5] + chain[2:4])
    ts(V("ncol", 0, 2), V("pos0", 1, 3), P * rank - 0.5, None, A.add)
    run(free[5:7] + chain[4:8])
    ts(V("negi", 0, 128), V("nat0", 0, 128), V("pr", 0, 1), -1.0, A.is_equal, A.mult)
    run(free[7:8] + chain[8:9] + free[8:] + chain[9:])
    signs(0, 0)
    signs(0, 1)

    early = (64, 160)
    flat = tables(1)
    flat += [(ms, V("sigm", 0, LM), 1.0), (ms, V("dgm", 32, 64), 0.0), (ms, V("dga", 32, 64), 0.0), (ms, V("trm", 32, 33), 256.0),
             (ms, V("fl", 0, 1), 0.0), (ms, V("sigm", 16, 17), 512.0)] + tail("eqm", 16, 0)
    flat += [(ts, V("eqm", 16, 17, 32 * i, 32 * i + 32), V("pf", 0, 1, 32 * i, 32 * i + 32), float(early[i]), None, A.add)
             for i in range(2)]
    flat += [(ts, V("idm", 0, 1), V("pf", 0, 1), 15.5, 64.0, A.is_gt, A.mult)]
    flat += [(ts, V("idm", 0, 1), V("idm", 0, 1), V("pf", 0, 1), None, A.add)]
    for c in (1, 2):
        flat.append((ms, V("nat%d" % c, 0, 32), -1.0 if rank >> (c - 1) & 1 else 5000.0))
    fills = [f for f in flat if f[0] is ms and f[2] == int(f[2]) and f[1][4] - f[1][3] <= 64]
    flat = [f for f in flat if f not in fills]
    soon, flat = flat[:3], flat[3:]
    spare = [[(ms, V("gh", 0, 192), LOW)]]
    spare += [[flat[i] for i in grp] for grp in ((0, 1, 2), (3, 14), (4, 5, 6), (7, 15), (8, 12, 13), (9,), (10, 11))]

    def between():
        if spare:
            run(spare.pop(0))

    def first_step(c):
        m, u, off = "m%d" % c, "u%d" % c, "off%d" % c
        low = rank >> (c - 1) & 1
        return [
            [(tt, V("dgm", 0, 32, 96 * i, 96 * i + 32), bank(5, 96 * i, 96 * i + 32, 96 * i, 96 * i + 32),
              V("negi", 96 * i, 96 * i + 32, 96 * i, 96 * i + 32), A.mult) for i in range(2)],
            [(scan, V("nbm", 0, 64, 32 - 32 * i, 64 - 32 * i), V("zero", 0, 64, 96 * i, 96 * i + 32),
              V("dgm", 0, 64, 96 * i, 96 * i + 32), A.add, A.add) for i in range(2)],
            [(tp, V("nrm", 0, 32, 0, 64), V("nbm", 32, 64, 0, 64))],
            [(ts, V("eqm", 0, 16, 32 * i, 32 * i + 32), V("nrm", 0, 16, 32 * i, 32 * i + 32),
              V("nbm", 63, 64, 32 - 32 * i, 64 - 32 * i), None, A.is_le if i == low else A.is_lt) for i in range(2)],
            [(scan, V("eom", 0, LM, 0, 64), V("sigm", 0, LM, 0, 64), V("eqm", 0, LM, 0, 64), A.mult, A.add, V("idm", 0, 1, 0, 64))],
            [(tp, V("trm", 0, 32, 0, 64), V("eom", 16, 48, 0, 64))]
            + [(ts, V("fl", 0, 1, 96 * i, 96 * i + 32), V("eom", 16, 17, 32 * i, 32 * i + 32), 8192.0, BIG, A.is_lt, A.mult)
               for i in range(2)],
            [(red, V("amm", 0, 1, 0, 64), V("trm", 0, 33, 0, 64), A.min, True)],
            [(ts, V(off, 0, 3, 32 * q, 32 * q + 32), V("cbm", 0, 3, 0, 32), V("amm", 0, 1, 0, 32), V("amm", 0, 1, 32, 64), A.add, A.add)
             for q in range(4)],
            [(pick, u, 0, m, 96, 128, V(off, 0, 1))]]

    def turn(z, i, k):
        w = 64 if i == 0 or z == 0 else 32
        po, pi = ((0, 128), (0, 64), (64, 128))[k], ((0, 128), (64, 128), (0, 64))[k]
        d = 128 * i + (w if k else 0)
        tp(V("nr", d, d + w, *po), V("nb", at(2 * i), at(2 * i) + w, *pi))

    def gram(c, b0, b1):
        n, starts, seq = shape[min(c, 1)][:3]
        for b, st in enumerate(starts):
            if b0 == 0:
                mm(b, n, "m%d" % c, 32 * st, "m%d" % c, 32)
        for b, st in list(enumerate(starts))[b0:b1]:
            ac(V("ga", b * n, b * n + n), bank(b, 0, n), F.Abs)
            q = 0
            while q < 4:
                e = q + 1
                while e < 4 and seq[st + e] == seq[st + e - 1] + 1:
                    e += 1
                c0 = b * n + 32 * seq[st + q]
                v = V("ga", c0, c0 + 32 * (e - q), 0, 32 * e)
                op("g", lambda: g.affine_select(ap(v), ap(v), [[-1, 32 * (e - q)]], A.not_equal, BIG, -32 * q, 1), [v], [v])
                q = e

    def choice(c):
        z = min(c, 1)
        n, starts, seq, ranked, part = shape[z]
        nw, t, L = len(starts), str(z), n + 33
        m, nx, off = "m%d" % c, "m%d" % (c + 1), "off%d" % c
        nat, natx, tnx = "nat%d" % c, "nat%d" % (c + 1), "tn%d" % (c + 1)
        last = c == 2
        place = (0, 32, 64) if last else (192, 160, 128)
        placen = place if last else (160, 128, 96)
        col = [V("nb", at(b), at(b) + 1) for b in ranked]
        peer, ar, ab = peers.get(c + 1), "ar%d" % (c + 1), "ab%d" % (c + 1)
        low = c and rank >> (c - 1) & 1 == 0

        def lst(s, k=1, b=0):
            c0 = (4 * s + b, 2 + 2 * s)[z]
            return V(off, c0, c0 + k)

        def winners(s, numbers=ac):
            d = 16 * (s % 2)
            pick(nx, place[s // 2] + d, m, 32, n, lst(s))
            o = V(natx, placen[s // 2] + d, placen[s // 2] + d + 16)
            if numbers is ac:
                ac(o, V(nat, 0, n), F.Identity, off=lst(s))
            else:
                cp(o, V(nat, 0, n), off=lst(s))

        def products(s, call):
            for o in range(O):
                y, a = V("ysb", W * o + 16 * s, W * o + 16 * s + 16), V("yall", n * o, n * o + n)
                if call is ac:
                    ac(y, a, F.Identity, off=lst(s))
                else:
                    cp(y, a, off=lst(s))

        for s in range(z, S):
            if s > z:
                if z == 0:
                    for i in range(2):
                        tt(V("gh", 96 * i + 32, 96 * i + 64), V("ga", 0, nw * n), V("nb", at(2 * i) + 16, at(2 * i) + 48), A.add,
                           off=lst(s - 1, 2, 2 * i))
                else:
                    for b in range(nw):
                        c0, d = 96 * (b // 2) + 32 + 16 * (b % 2), at(b) + 16 - 16 * (b % 2)
                        tt(V("gh", c0, c0 + 16), V("ga", b * n, b * n + n), V("nb", d, d + 16), A.add, off=lst(s - 1))
                for b in range(nw):
                    c0 = 96 * (b // 2) + 48 * (b % 2)
                    scan(into(b, 16), V("zero", 0, 48), V("gh", c0, c0 + 48, step=2 * (b % 2) - 1), A.add, A.max, LOW)
                winners(s - 1)
                if last and s == 2:
                    repeat(nx, 96, 0, "da3")
                    repeat(nx, 64, 0, "db3")
                elif last and s == 4:
                    mm(6, P, nx, 0, "m0", 32)
                    dma("y", T.oc[:, 0:256], V(nx + "q", 0, 64))
                elif s == 2:
                    send(peer, [(V(nx + "q", 96, 128), V(nx + "q", 192, 224))], ab)
                    send(peer, [(V(nx + "s", 96, 128), V(nx + "s", 192, 224))], ab)
                    repeat(nx, 160, 192, "dc%d" % (c + 1))
                    repeat(nx, 128, 192, "dd%d" % (c + 1))
                    repeat(nx, 224, 192, "da%d" % (c + 1))
                    repeat("u%d" % (c + 1), 16, 32, "du%d" % (c + 1), "m0", 112)
                elif s == 4:
                    repeat(nx, 0, 160, "db%d" % (c + 1))
                    send(peer, [(V(nx + "q", 64, 96), V(nx + "q", 160, 192))], ar)
                elif s == 5 and not last:
                    send(peer, [(V(nx + "q", 32, 48), V(nx + "q", 128, 144))], ar)
            for i in range(2):
                for k in range(3):
                    turn(z, i, k)
            for a in range(2):
                lo, hi = part[a]
                ac(V("junk", 256 * a, 256 * a + hi - lo), V("nr", lo, hi), F.Sign, bias=col[a], accum=V("acc", a, a + 1))
            if s == z:
                gram(c, nw - 1, nw)
            (l0, h0), (l1, h1) = part
            ts(V("eq" + t, l0, h0), V("nr", l0, h0), col[0], None, A.is_equal)
            ts(V("eq" + t, L, L + l1), V("nr", 0, l1), col[1], None, A.is_lt if low else A.is_le)
            if s == z and c:
                multipliers(c, 0)
            ts(V("eq" + t, h0, n), V("nr", h0, n), col[0], None, A.is_le if low else A.is_lt)
            ts(V("eq" + t, L + l1, L + n), V("nr", l1, n), col[1], None, A.is_equal)
            for a in range(2):
                scan(V("eo", a * L, a * L + L, step=1 - 2 * a), V("sig" + t, a * L, a * L + L), V("eq" + t, a * L, a * L + L),
                     A.mult, A.add, V("acc", a, a + 1))
            if s == 0:
                run(soon)
                for f in fills:
                    iota(f[1], [[0, f[1][4] - f[1][3]]], int(f[2]), 0)
            elif c == 2 and s == 1:
                winners(0)
                for o in range(O):
                    mm(3 + o, n, "w", 128 * o, m, 32)
            elif c == 1 and s == 1:
                winners(0)
            elif c == 1 and s == 2:
                quant("w", "wt", 0, 128)
            elif s == 4 and not last:
                tp(V(tnx, 0, 64), V(natx, 128, 192))
            else:
                between()
            if last and s == 2:
                for o in range(O):
                    ac(V("yall", n * o, n * o + n), bank(3 + o, 0, n), F.Identity)
            if last and s == 4:
                ac(V("zsb", 0, P, 0, 64), bank(6, 0, P, 0, 64), F.Copy)
                dma("y", T.z[0:64, :], V("zsb", 0, P, 0, 64))
            if last and s >= 3:
                for k in ((0, 1), (2, 3), (4,))[s - 3]:
                    products(k, ac)
                if s == 5:
                    for o in range(O):
                        dma("y", T.y[:, W * o:W * o + 80], V("ysb", W * o, W * o + 80))
            if z == 0:
                for h in range(2):
                    tp(V("tr0", 64 * h, 64 * h + 64, 0, 64), V("eo", L - 32, L + 32, 64 * h, 64 * h + 64))
            else:
                tp(V("tr1", 0, 64, 0, 96), V("eo", L - 32, L + 32, 0, 96))
            if s == 3 and not last:
                mm(5, 128, nx, 96, nx, 96)
                assert not spare
                spare.extend(first_step(c + 1))
            if s == 4 and not last:
                cp(V("sa%d" % (c + 1), 0, 2), V(tnx, 0, 64, step=32))
                send(peer, [(V("la%d" % (c + 1), 0, 2), V("sa%d" % (c + 1), 0, 2))], "ae%d" % (c + 1))
            if c == 1 and s == 2:
                quant("w", "wt", 128, 256)
            else:
                between()
            if z == 0:
                red(V("am", 0, 1, 0, 64), V("tr0", 0, 129, 0, 64), A.min, True)
            else:
                red(V("am", 0, 1, 0, 96), V("tr1", 0, 64, 0, 96), A.min, True)
            if c == 1 and s == 2:
                quant("w", "wt", 256, 384)
            else:
                between()
            for q in range(4):
                o = lst(s, nw) if z == 0 else lst(s)
                o = V(off, o[3], o[4], 32 * q, 32 * q + 32)
                if z == 0:
                    ts(o, V("cb0", 0, 4, 0, 32), V("am", 0, 1, 0, 32), V("am", 0, 1, 32, 64), A.add, A.add)
                else:
                    ts(o, V("am", 0, 1, 0, 32), V("am", 0, 1, 32, 64), V("am", 0, 1, 64, 96), A.min, A.min)
            if s < 5:
                between()

        if last:
            pick(nx, 80, m, 32, n, lst(5))
            products(5, cp)
            ac(V(natx, 80, 96), V(nat, 0, n), F.Identity, off=lst(5))
            return
        c += 1
        u, la, ln = "u%d" % c, "la%d" % c, "ln%d" % c
        winners(5, cp)
        send(peer, [(V(nx + "q", 48, 64), V(nx + "q", 144, 160)), (V(nx + "s", 32, 96), V(nx + "s", 128, 192))], ar)
        while spare:
            between()
        cp(V("lf", 0, 2), V(la, 0, 2))
        tp(V(tnx, 64, 96), V(natx, 96, 128))
        send(peer, [(V(ln, 0, 1), V(tnx, 64, 65))], "an%d" % c)
        mm(6, 128, nx, 96, nx, 96)
        mm(7, 128, nx, 96, u, 0)
        for i in range(2):
            ts(V("pn", 32 + 32 * i, 64 + 32 * i), V("zero", 0, 32), V("lf", i, i + 1), None, A.add)
        ts(V("ncol", 1, 2, 32, 64), V(tnx, 0, 1, 32, 64), -0.5, None, A.add)
        ts(V("ncol", 1, 2, 64, 128), V(tnx, 32, 33, 64, 128), -0.5, None, A.add)
        ts(V("ncol", 1, 2, 0, 32), V(tnx, 64, 65, 0, 32), -0.5, None, A.add)
        tp(V(natx, 32, 96), V("pn", 32, 96))
        tt(V("dgy", 0, 128), bank(6, 0, 128), V("negi", 0, 128), A.mult)
        signs(c, 1)
        red(V("dy", 0, 1), bank(7, 0, 16), A.max, True)
        ts(V("ncol", 0, 1, 32, 64), V("lf", 0, 1, 32, 64), -0.5, None, A.add)
        ts(V("ncol", 0, 1, 64, 96), V("lf", 1, 2, 64, 96), -0.5, None, A.add)
        red(V("dy", 1, 2), V("dgy", 0, 128), A.add)
        multipliers(c, 1)
        ts(V("dy", 2, 3), V("dy", 1, 2), V("fl", 0, 1), None, A.add)
        for b, p0, p1, s0 in ((0, 64, 128, 0), (1, 0, 32, 64), (1, 96, 128, 0), (2, 0, 32, 32), (2, 32, 64, 64), (2, 64, 96, 96),
                              (2, 96, 128, 96)):
            s1 = s0 + p1 - p0
            ts(block(b, p0, p1), V("zero", 0, 32, p0, p1), V("dy", 0, 1, s0, s1), V("dy", 2, 3, s0, s1), A.add, A.add)
        mm(3, 128, nx, 32, nx, 32)
        mm(4, 128, nx, 32, u, 0)
        for q in range(2):
            tt(V("dga", 0, 32, 32 * q, 32 * q + 32), bank(3, 32 * q, 32 * q + 32, 32 * q, 32 * q + 32),
               V("negi", 32 * q, 32 * q + 32, 32 * q, 32 * q + 32), A.mult)
        red(V("dy", 3, 4, 0, 64), bank(4, 0, 16, 0, 64), A.max, True)
        ts(V("pn", 0, 32), V("zero", 0, 32), V(ln, 0, 1), None, A.add)
        ts(V("ncol", 0, 1, 0, 32), V(ln, 0, 1, 0, 32), -0.5, None, A.add)
        for b, p0, p1, s0 in ((0, 0, 64, 0), (1, 32, 64, 0), (1, 64, 96, 32)):
            s1 = s0 + p1 - p0
            scan(into(b, 32, p0, p1), V("zero", 0, 64, s0, s1), V("dga", 0, 64, s0, s1), A.add, A.add, V("dy", 3, 4, s0, s1))
        gram(c, 0, 2)
        tp(V(natx, 0, 32), V("pn", 0, 32))
        signs(c, 0)

    for h in range(2):
        quant("m0", "xt", 160 * h, 160 * h + 160)
        for b in (2 * h, 2 * h + 1):
            mm(4 + b, 128, "m0", 32 * shape[0][1][b], "m0", 32 * shape[0][1][b])
    gram(0, 0, 3)
    run(late)
    for h in range(2):
        for b in (2 * h, 2 * h + 1):
            c0 = 320 * h + 192 * (b % 2)
            tt(V("dgo", c0, c0 + 128), bank(4 + b, 0, 128), V("negi", 0, 128), A.mult)
        multipliers(0, h)
        for b in (2 * h, 2 * h + 1):
            c0 = 320 * h + 160 * (b % 2)
            scan(into(b, 128), V("zero", 0, 160), V("dgo", c0, c0 + 160, step=1 - 2 * (b % 2)), A.add, A.add)

    for c in range(3):
        choice(c)

    def scales_out(q, k):
        dma(q, T.osc[4 * k:4 * k + 4, :], V("m3s", 0, W, 32 * k, 32 * k + 4))

    for h in range(2):
        mm(6 + h, 128, "m3", 0, "m0", 32 + 128 * h)
    dma("y", T.oc[:, 256:4 * W], V("m3q", 64, W))
    scales_out("s", 0)
    scales_out("s", 1)
    for o in range(O):
        dma("y", T.y[:, W * o + 80:W * o + W], V("ysb", W * o + 80, W * o + W))
    dma("s", T.wn[:], V("nat3", 0, W, 0, 1))
    ac(V("zsb", 128, P, 64, W), bank(7, 0, 128, 64, W), F.Copy)
    cp(V("zsb", 0, 128, 64, W), bank(6, 0, 128, 64, W))
    scales_out("y", 2)
    scales_out("y", 3)
    dma("s", T.z[64:W, :], V("zsb", 0, P, 64, W))
    g.sync.wait_ge(T.sem.st, count["st"])
    g.wait_ge(T.sem.sent, sent[0])
    for k in own_sem:
        wait("y", (own_sem[k], count[own_sem[k]], {}))
